import numpy as np
import ml_dtypes


def mxq(x, axis, fmt="e4m3"):
    dtype, down = {"e4m3": (ml_dtypes.float8_e4m3fn, 7), "e5m2": (ml_dtypes.float8_e5m2, 14)}[fmt]
    v = np.moveaxis(np.asarray(x, np.float32).astype(ml_dtypes.bfloat16).astype(np.float64), axis, -1)
    blocks = v.reshape(v.shape[:-1] + (-1, 32))
    amax = np.abs(blocks).max(-1, keepdims=True)
    byte = np.maximum(np.where(amax > 0, np.frexp(amax)[1] - 1 + 127, 0) - down, 1)
    scale = np.exp2(byte - 127.0)
    codes = (blocks / scale).astype(np.float32).astype(dtype).astype(np.float64)
    return np.moveaxis((codes * scale).reshape(v.shape), -1, axis)


WIDE = False


def mx_kscale(k):
    if not WIDE:
        return np.ones(k)
    levels = np.array([10, -10, 5, -5, 0])
    if k % 512:
        return np.exp2(np.random.permutation(np.resize(levels, k // 32))).repeat(32)
    a = np.empty((k // 512, 16))
    for p in range(k // 512):
        a[p, :8] = np.random.permutation(np.resize(levels, 8))
        for g in range(8):
            far = levels[np.abs(levels - a[p, g]) >= 10]
            a[p, g + 8] = far[np.random.randint(len(far))]
    return np.exp2(a.ravel()).repeat(32)


def f64(x):
    return np.asarray(x).astype(np.float64)


def striped(idx):
    return np.tile(idx.reshape(-1, 16).T, (8, 1)).astype(np.uint16)


def unstriped(offs):
    return offs[:16].T.reshape(-1).astype(np.int64)


E2M1 = np.array([0.0, 0.5, 1.0, 1.5, 2.0, 3.0, 4.0, 6.0, -0.0, -0.5, -1.0, -1.5, -2.0, -3.0, -4.0, -6.0])


def pack_weight(w, fmt):
    k, n = w.shape
    w = f64(np.asarray(w, np.float32).astype(ml_dtypes.bfloat16)).reshape(k // 32, 32, n)
    amax = np.abs(w).max(1)
    if fmt == "e4m3":
        byte = np.frexp(amax)[1] - 1 + 127 - 7
    else:
        mant, ex = np.frexp(amax / 6.0)
        byte = np.where(mant > 0.5, ex, ex - 1) + 127
    byte = np.clip(np.where(amax > 0, byte, 1), 1, 254)
    scaled = (w * np.exp2(127.0 - byte)[:, None, :]).reshape(k, n).astype(np.float32)
    by_word = np.ascontiguousarray(scaled.reshape(k // 512, 128, 4, n).transpose(0, 1, 3, 2))
    if fmt == "e4m3":
        words = by_word.astype(ml_dtypes.float8_e4m3fn).view(np.uint8)
    else:
        c = by_word.astype(ml_dtypes.float4_e2m1fn).view(np.uint8) & 0xF
        words = (c[..., 0::2] | (c[..., 1::2] << 4)).reshape(k // 512, 128, 2 * n)
    return np.ascontiguousarray(words), np.ascontiguousarray(byte.astype(np.uint8).reshape(k // 512, 16, n))


def unpack_weight(words, scales, fmt):
    g, _, n = scales.shape
    words = np.ascontiguousarray(words).reshape(g, 128, n, -1)
    if fmt == "e4m3":
        vals = words.view(ml_dtypes.float8_e4m3fn).astype(np.float64)
    else:
        nib = np.empty((g, 128, n, 4), np.uint8)
        nib[..., 0::2] = words & 0xF
        nib[..., 1::2] = words >> 4
        vals = E2M1[nib]
    vals = vals * np.repeat(np.exp2(scales.astype(np.float64) - 127.0), 8, axis=1)[..., None]
    return vals.transpose(0, 1, 3, 2).reshape(g * 512, n)


def gelu(v):
    return 0.5 * v * (1.0 + np.tanh(np.sqrt(2.0 / np.pi) * (v + 0.044715 * v**3)))


def bf(x):
    return np.asarray(x, np.float32).astype(ml_dtypes.bfloat16)

def planes(Y):
    n, m = Y.shape
    b = f64(bf(Y)).reshape(n // 32, 32, m)
    amax = np.abs(b).max(1)
    byte = np.clip(np.where(amax > 0, np.frexp(amax)[1] - 1 + 127 - 7, 1), 1, 254)
    codes = (b * np.exp2(127.0 - byte)[:, None, :]).reshape(n, m).astype(np.float32).astype(ml_dtypes.float8_e4m3fn).view(np.uint8)
    words = codes.reshape(n // 512, 128, 4, m).transpose(0, 1, 3, 2)
    return np.ascontiguousarray(words), np.ascontiguousarray(byte.astype(np.uint8).reshape(n // 512, 16, m))


K, T, S, H, N = 1024, 2048, 1024, 512, 1024

def setup_inputs():
    n = np.random.standard_normal
    s = mx_kscale(K)[:, None]
    u = mx_kscale(H)[:, None]
    cap = np.exp(0.3 * n(H)) * u[:, 0]
    tab_words, tab_scales = pack_weight((0.5 + n((K, T))) * s, "e4m3")
    tab2_words, tab2_scales = pack_weight((0.5 + n((K, T))) * s, "e4m3")
    wo = (0.8 * n((K, H)) + 1 / np.sqrt(K)) / np.sqrt(K) / s
    wo_words, wo_scales = pack_weight(wo, "e2m1")
    wp = (0.8 * n((K, H)) + 1 / np.sqrt(K)) / np.sqrt(K) / s * cap[None, :]
    we = 2.0 * n((H, N)) / np.sqrt(H) / u * np.exp(0.8 * n(N))[None, :]
    return {
        "tab_words": tab_words, "tab_scales": tab_scales,
        "tab2_words": tab2_words, "tab2_scales": tab2_scales,
        "offs": striped(np.random.permutation(T)[:S]),
        "offs2": striped(np.random.permutation(T)[:S]),
        "wo_words": wo_words, "wo_scales": wo_scales,
        "wp": wp.astype(np.float32), "cap": cap.astype(np.float32),
        "we": we.astype(np.float32),
    }

def reference(tab_words, tab_scales, tab2_words, tab2_scales, offs, offs2, wo_words, wo_scales, wp, cap, we):
    v = unpack_weight(tab_words, tab_scales, "e4m3")[:, unstriped(offs)]
    v2 = unpack_weight(tab2_words, tab2_scales, "e4m3")[:, unstriped(offs2)]
    wo = unpack_weight(wo_words, wo_scales, "e2m1")
    a = wo.T @ v
    b = mxq(f64(wp), 0, "e4m3").T @ v2
    own = np.minimum(np.maximum(a, 0.0), 1.0)
    opp = np.minimum(np.maximum(b, 0.0), f64(cap)[:, None])
    h = own * opp
    y = mxq(f64(we), 0, "e4m3").T @ mxq(h, 0, "e4m3")
    words, scales = planes(y)
    return y, words, scales

@@ -1,0 +1,286 @@
+from contextlib import ExitStack
+
+import concourse.mybir as mybir
+
+K, T, S, H, N = 1024, 2048, 1024, 512, 1024
+FLOPS = 2 * (2 * K * H * S + H * N * S)
+
+F32 = mybir.dt.float32
+BF16 = mybir.dt.bfloat16
+I32 = mybir.dt.int32
+U32 = mybir.dt.uint32
+U16 = mybir.dt.uint16
+U8 = mybir.dt.uint8
+FP8X4 = mybir.dt.float8_e4m3fn_x4
+FP4X4 = mybir.dt.float4_e2m1fn_x4
+ALU = mybir.AluOpType
+RELU = mybir.ActivationFunctionType.Relu
+
+P = 128
+PACK = 4
+PASSES = K // (P * PACK)
+GROUPS = N // (P * PACK)
+UNIT = 128
+UNITS = S // UNIT
+HALF = S // 2
+QUARTER = S // 4
+ROW0 = 96
+SCALAR_ROUNDS = ((0, 1), (1, 1), (2, 1))
+
+
+def tile_list_clamped_pair_eval_kernel(
+    tc, tab_words, tab_scales, tab2_words, tab2_scales, offs, offs2, wo_words, wo_scales, wp, cap, we, out_0, out_1, out_2
+):
+    nc = tc.nc
+    with ExitStack() as ctx:
+        lists = ctx.enter_context(tc.tile_pool(name="lists", bufs=1))
+        keep = ctx.enter_context(tc.tile_pool(name="keep", bufs=1))
+        ring = ctx.enter_context(tc.tile_pool(name="ring", bufs=3))
+        psum = ctx.enter_context(tc.psum_pool(name="psum", bufs=4))
+
+        offsets = [lists.tile([P, S // 16], U16, name=f"offsets{s}") for s in range(2)]
+        scale_window = [keep.tile([P, T], U8, name=f"scale_window{s}", align_bytes=64) for s in range(2)]
+        scale_picked = [keep.tile([P, S], U8, name=f"scale_picked{s}", align_bytes=64) for s in range(2)]
+        v_scales = keep.tile([P, PASSES * S], U8, align_bytes=64)
+        word_window = [[keep.tile([P, T], U32, name=f"word_window{s}{a}", align_bytes=64) for a in range(PASSES)] for s in range(2)]
+        v_words = [
+            [[keep.tile([P, HALF], U32, name=f"v_words{s}{a}{hf}", align_bytes=64) for hf in range(2)] for a in range(PASSES)]
+            for s in range(2)
+        ]
+        wo_raw = keep.tile([P, PASSES * 2 * H], U8, align_bytes=64)
+        wo_scale_raw = keep.tile([P, PASSES * H], U8, align_bytes=64)
+        wo_codes = keep.tile([P, PASSES * 2 * H], U8, align_bytes=64)
+        wo_plane = keep.tile([P, PASSES * H], U8, align_bytes=64)
+        wp_raw = [keep.tile([P, PACK, H], F32, name=f"wp_raw{a}") for a in range(PASSES)]
+        wp_round = [keep.tile([P, PACK * H], BF16, name=f"wp_round{a}", align_bytes=64) for a in range(PASSES)]
+        wp_codes = [keep.tile([P, H], U32, name=f"wp_codes{a}", align_bytes=64) for a in range(PASSES)]
+        wp_plane = [keep.tile([P, H], U8, name=f"wp_plane{a}", align_bytes=64) for a in range(PASSES)]
+        we_raw = [keep.tile([P, PACK, 512], F32, name=f"we_raw{g}") for g in range(GROUPS)]
+        we_round = [keep.tile([P, PACK * 512], BF16, name=f"we_round{g}", align_bytes=64) for g in range(GROUPS)]
+        we_codes = [keep.tile([P, 512], U32, name=f"we_codes{g}", align_bytes=64) for g in range(GROUPS)]
+        we_plane = [keep.tile([P, 512], U8, name=f"we_plane{g}", align_bytes=64) for g in range(GROUPS)]
+        cap_raw = keep.tile([P, PACK, 8], F32)
+        cap_col = keep.tile([P, PACK], F32)
+        own = [keep.tile([P, UNIT * PACK], F32, name=f"own{u}") for u in range(UNITS)]
+        h_codes = keep.tile([P, S], U32, align_bytes=64)
+        h_plane = keep.tile([P, S], U8, align_bytes=64)
+        y_full = [[keep.tile([P, PACK, QUARTER], F32, name=f"y_full{q}{g}") for g in range(GROUPS)] for q in range(4)]
+        y_round = [[keep.tile([P, QUARTER * PACK], BF16, name=f"y_round{q}{g}", align_bytes=64) for g in range(GROUPS)] for q in range(4)]
+        y_codes = [keep.tile([P, S], U32, name=f"y_codes{g}", align_bytes=64) for g in range(GROUPS)]
+        y_plane = keep.tile([P, GROUPS * S], U8, align_bytes=64)
+
+        words_in = (tab_words, tab2_words)
+
+        nc.vector.memset(scale_window[1][:].bitcast(I32), 0)
+        nc.vector.memset(wo_scale_raw[:].bitcast(I32), 0)
+        nc.vector.memset(v_scales[:].bitcast(I32), 0)
+
+        def load_words(s, a):
+            nc.sync.dma_start(word_window[s][a][:].bitcast(I32), words_in[s][a].rearrange("p t i -> p (t i)").bitcast(I32))
+
+        def load_wp(a):
+            nc.sync.dma_start(wp_raw[a][:], wp[a * 512 : (a + 1) * 512, :].rearrange("(p j) c -> p j c", j=PACK))
+
+        def load_we(g):
+            rows = we.rearrange("(q j i) n -> j q i n", j=PACK, i=8)
+            for j in range(PACK):
+                nc.sync.dma_start(we_raw[g][:, j, :], rows[j][:, :, g * 512 : (g + 1) * 512])
+
+        nc.sync.dma_start(offsets[0][:], offs)
+        nc.sync.dma_start(scale_window[0][ROW0:P, :].bitcast(I32), tab_scales.bitcast(I32).rearrange("a q t -> q a t"))
+        nc.vector.memset(scale_window[0][0:ROW0, :].bitcast(I32), 0)
+        nc.sync.dma_start(offsets[1][:], offs2)
+        load_wp(0)
+        for quad in range(4):
+            nc.scalar.dma_start(
+                scale_window[1][32 * quad : 32 * quad + 8, :].bitcast(I32), tab2_scales.bitcast(I32)[:, 4 * quad : 4 * quad + 4, :]
+            )
+        load_words(0, 0)
+        nc.sync.dma_start(
+            wo_raw[:].bitcast(I32).rearrange("p (a w) -> p a w", a=PASSES), wo_words.bitcast(I32).rearrange("a p w -> p a w")
+        )
+        wo_scale_rows = wo_scales.bitcast(I32).rearrange("a q w -> q a w")
+        for quad in range(4):
+            nc.scalar.dma_start(
+                wo_scale_raw[32 * quad : 32 * quad + 4, :].bitcast(I32).rearrange("p (a w) -> p a w", a=PASSES),
+                wo_scale_rows[4 * quad : 4 * quad + 4],
+            )
+        load_wp(1)
+        load_words(0, 1)
+        load_words(1, 0)
+        load_words(1, 1)
+        cap_rows = cap.rearrange("(q t i o) -> t q i o", t=PACK, i=8, o=1)
+        for t in range(PACK):
+            nc.gpsimd.dma_start(cap_raw[:, t, 0:1], cap_rows[t])
+        load_we(0)
+        load_we(1)
+
+        def gather_scales(s):
+            nc.vector.tensor_copy(scale_picked[s][:], scale_window[s][:].indirect(offsets[s][:]))
+
+        def gather_words(s, a, hf):
+            cols = slice(hf * HALF // 16, (hf + 1) * HALF // 16)
+            nc.vector.tensor_copy(v_words[s][a][hf][:], word_window[s][a][:].indirect(offsets[s][:, cols]))
+
+        def round_wp(a):
+            nc.scalar.copy(
+                wp_round[a][:].rearrange("p (t q i j) -> p t q i j", t=PACK, i=8, j=PACK),
+                wp_raw[a][:].rearrange("p j (q t i) -> p t q i j", t=PACK, i=8),
+            )
+
+        def round_we(g):
+            nc.scalar.copy(
+                we_round[g][:].rearrange("p (t m j) -> p m t j", t=PACK, j=PACK),
+                we_raw[g][:].rearrange("p j (m t) -> p m t j", t=PACK),
+            )
+
+        def quantise(codes, plane, values):
+            nc.vector.quantize_mx(out=codes.bitcast(FP8X4), scales=plane, in_=values)
+
+        def deal_wo():
+            nc.vector.tensor_copy(
+                wo_codes[:].bitcast(I32).rearrange("p (a t q w) -> p a t q w", a=PASSES, t=PACK, w=4),
+                wo_raw[:].bitcast(I32).rearrange("p (a q t w) -> p a t q w", a=PASSES, t=PACK, w=4),
+            )
+            nc.vector.tensor_copy(
+                wo_plane[:].bitcast(I32).rearrange("p (a t q w) -> p a t q w", a=PASSES, t=PACK, w=2),
+                wo_scale_raw[:].bitcast(I32).rearrange("p (a q t w) -> p a t q w", a=PASSES, t=PACK, w=2),
+            )
+
+        def project(s, u):
+            bank = psum.tile([P, PACK, UNIT], F32, name="project_bank")
+            hf, c0 = divmod(u * UNIT, HALF)
+            for t in range(PACK):
+                for a in range(PASSES):
+                    if s == 0:
+                        lo = a * H + t * P
+                        weights, weight_plane = wo_codes[:, 2 * lo : 2 * (lo + P)].bitcast(FP4X4), wo_plane[:, lo : lo + P]
+                        table_plane = v_scales[:, a * S + u * UNIT : a * S + (u + 1) * UNIT]
+                    else:
+                        weights, weight_plane = wp_codes[a][:, t * P : (t + 1) * P].bitcast(FP8X4), wp_plane[a][:, t * P : (t + 1) * P]
+                        table_plane = scale_picked[1][4 * a : P, u * UNIT : (u + 1) * UNIT]
+                    nc.tensor.matmul_mx(
+                        out=bank[:, t, :],
+                        lhsT=weights,
+                        lhsT_scale=weight_plane,
+                        rhs=v_words[s][a][hf][:, c0 : c0 + UNIT].bitcast(FP8X4),
+                        rhs_scale=table_plane,
+                        start=(a == 0),
+                        stop=(a == PASSES - 1),
+                    )
+            return bank
+
+        def own_side(u):
+            bank = project(0, u)
+            nc.scalar.activation(own[u][:].rearrange("p (c t) -> p c t", t=PACK), bank[:].rearrange("p t c -> p c t"), RELU)
+
+        opp = {}
+        h_round = {}
+
+        def opponent_side(u):
+            bank = project(1, u)
+            opp[u] = ring.tile([P, UNIT * PACK], F32, name="opp")
+            nc.vector.scalar_tensor_tensor(
+                out=opp[u][:].rearrange("p (c t) -> p c t", t=PACK),
+                in0=bank[:].rearrange("p t c -> p c t"),
+                scalar=0.0,
+                in1=cap_col[:].unsqueeze(1).to_broadcast([P, UNIT, PACK]),
+                op0=ALU.max,
+                op1=ALU.min,
+            )
+
+        def combine(u):
+            h_round[u] = ring.tile([P, UNIT * PACK], BF16, name="h_round", align_bytes=64)
+            nc.vector.scalar_tensor_tensor(out=h_round[u][:], in0=own[u][:], scalar=1.0, in1=opp[u][:], op0=ALU.min, op1=ALU.mult)
+
+        def quantise_h(u):
+            cols = slice(u * UNIT, (u + 1) * UNIT)
+            quantise(h_codes[:, cols], h_plane[:, cols], h_round[u][:])
+
+        def evaluate(u, g):
+            q, c0 = divmod(u * UNIT, QUARTER)
+            cols = slice(u * UNIT, (u + 1) * UNIT)
+            bank = psum.tile([P, PACK, UNIT], F32, name="evaluate_bank")
+            for t in range(PACK):
+                nc.tensor.matmul_mx(
+                    out=bank[:, t, :],
+                    lhsT=we_codes[g][:, t * P : (t + 1) * P].bitcast(FP8X4),
+                    lhsT_scale=we_plane[g][:, t * P : (t + 1) * P],
+                    rhs=h_codes[:, cols].bitcast(FP8X4),
+                    rhs_scale=h_plane[:, cols],
+                    start=True,
+                    stop=True,
+                )
+            nc.scalar.copy(y_full[q][g][:, :, c0 : c0 + UNIT], bank[:])
+            if (q, g) in SCALAR_ROUNDS:
+                nc.scalar.copy(
+                    y_round[q][g][:, PACK * c0 : PACK * (c0 + UNIT)].rearrange("p (c t) -> p c t", t=PACK),
+                    bank[:].rearrange("p t c -> p c t"),
+                )
+
+        def store_y(q, g):
+            rows = out_0[g * 512 : (g + 1) * 512, q * QUARTER : (q + 1) * QUARTER]
+            nc.sync.dma_start(rows.rearrange("(p t) c -> p t c", t=PACK), y_full[q][g][:])
+
+        def round_y(q, g):
+            if (q, g) not in SCALAR_ROUNDS:
+                nc.vector.tensor_copy(
+                    y_round[q][g][:].rearrange("p (c t) -> p c t", t=PACK), y_full[q][g][:].rearrange("p t c -> p c t")
+                )
+
+        def quantise_y(q, g):
+            cols = slice(q * QUARTER, (q + 1) * QUARTER)
+            quantise(y_codes[g][:, cols], y_plane[:, g * S + q * QUARTER : g * S + (q + 1) * QUARTER], y_round[q][g][:])
+            nc.sync.dma_start(out_1[g].rearrange("p m t -> p (m t)").bitcast(I32)[:, cols], y_codes[g][:, cols].bitcast(I32))
+
+        gather_scales(0)
+        for quad in range(4):
+            nc.gpsimd.dma_start(
+                v_scales[32 * quad : 32 * quad + 4, :].bitcast(I32).rearrange("p (a w) -> p a w", a=PASSES),
+                scale_picked[0][ROW0 + 8 * quad : ROW0 + 8 * quad + 8, :].bitcast(I32),
+            )
+        round_wp(0)
+        gather_scales(1)
+        gather_words(0, 0, 0)
+        gather_words(0, 0, 1)
+        deal_wo()
+        quantise(wp_codes[0][:], wp_plane[0][:], wp_round[0][:])
+        round_wp(1)
+        for hf in range(2):
+            gather_words(0, 1, hf)
+            for u in range(4 * hf, 4 * hf + 4):
+                own_side(u)
+        quantise(wp_codes[1][:], wp_plane[1][:], wp_round[1][:])
+        nc.vector.tensor_copy(cap_col[:], cap_raw[:, :, 0])
+        gather_words(1, 0, 0)
+        gather_words(1, 1, 0)
+        gather_words(1, 0, 1)
+        gather_words(1, 1, 1)
+        for g in range(GROUPS):
+            round_we(g)
+            quantise(we_codes[g][:], we_plane[g][:], we_round[g][:])
+
+        for step in range(UNITS + 6):
+            if step < UNITS:
+                opponent_side(step)
+            if 0 <= step - 1 < UNITS:
+                combine(step - 1)
+            if 0 <= step - 2 < UNITS:
+                quantise_h(step - 2)
+                for g in range(GROUPS):
+                    evaluate(step - 2, g)
+            if 0 <= step - 3 < UNITS and (step - 3) % 2 == 1:
+                for g in range(GROUPS):
+                    store_y((step - 3) // 2, g)
+                    round_y((step - 3) // 2, g)
+            if 0 <= step - 4 < UNITS and (step - 4) % 2 == 1:
+                for g in range(GROUPS):
+                    quantise_y((step - 4) // 2, g)
+
+        scale_rows = out_2.bitcast(I32).rearrange("g q w -> q g w")
+        for quad in range(4):
+            queue = nc.sync if quad % 2 == 0 else nc.scalar
+            queue.dma_start(
+                scale_rows[4 * quad : 4 * quad + 4],
+                y_plane[32 * quad : 32 * quad + 4, :].bitcast(I32).rearrange("p (g w) -> p g w", g=GROUPS),
+            )

@@ -23,9 +23,10 @@ GROUPS = N // (P * PACK)
 UNIT = 128
 UNITS = S // UNIT
 HALF = S // 2
-QUARTER = S // 4
+PIECES = ((0, 2), (2, 2), (4, 2), (6, 2))
 ROW0 = 96
-SCALAR_ROUNDS = ((0, 1), (1, 1), (2, 1))
+CODE_STORES = {4: 0, 8: 4}
+SCALAR_ROUNDS = ((0, 0), (2, 0), (2, 1))
 
 
 def tile_list_clamped_pair_eval_kernel(
@@ -41,7 +42,7 @@ def tile_list_clamped_pair_eval_kernel(
         offsets = [lists.tile([P, S // 16], U16, name=f"offsets{s}") for s in range(2)]
         scale_window = [keep.tile([P, T], U8, name=f"scale_window{s}", align_bytes=64) for s in range(2)]
         scale_picked = [keep.tile([P, S], U8, name=f"scale_picked{s}", align_bytes=64) for s in range(2)]
-        v_scales = keep.tile([P, PASSES * S], U8, align_bytes=64)
+        v_scales = [keep.tile([P, PASSES * S], U8, name=f"v_scales{s}", align_bytes=64) for s in range(2)]
         word_window = [[keep.tile([P, T], U32, name=f"word_window{s}{a}", align_bytes=64) for a in range(PASSES)] for s in range(2)]
         v_words = [
             [[keep.tile([P, HALF], U32, name=f"v_words{s}{a}{hf}", align_bytes=64) for hf in range(2)] for a in range(PASSES)]
@@ -64,16 +65,20 @@ def tile_list_clamped_pair_eval_kernel(
         own = [keep.tile([P, UNIT * PACK], F32, name=f"own{u}") for u in range(UNITS)]
         h_codes = keep.tile([P, S], U32, align_bytes=64)
         h_plane = keep.tile([P, S], U8, align_bytes=64)
-        y_full = [[keep.tile([P, PACK, QUARTER], F32, name=f"y_full{q}{g}") for g in range(GROUPS)] for q in range(4)]
-        y_round = [[keep.tile([P, QUARTER * PACK], BF16, name=f"y_round{q}{g}", align_bytes=64) for g in range(GROUPS)] for q in range(4)]
+        y_full = {q: [keep.tile([P, PACK, n * UNIT], F32, name=f"y_full{q}{g}") for g in range(GROUPS)] for q, n in PIECES}
+        y_round = {q: [keep.tile([P, n * UNIT * PACK], BF16, name=f"y_round{q}{g}", align_bytes=64) for g in range(GROUPS)] for q, n in PIECES}
         y_codes = [keep.tile([P, S], U32, name=f"y_codes{g}", align_bytes=64) for g in range(GROUPS)]
         y_plane = keep.tile([P, GROUPS * S], U8, align_bytes=64)
 
         words_in = (tab_words, tab2_words)
 
-        nc.vector.memset(scale_window[1][:].bitcast(I32), 0)
-        nc.vector.memset(wo_scale_raw[:].bitcast(I32), 0)
-        nc.vector.memset(v_scales[:].bitcast(I32), 0)
+        scales_in = (tab_scales, tab2_scales)
+        lists_in = (offs, offs2)
+
+        def load_list_and_scales(s):
+            nc.sync.dma_start(offsets[s][:], lists_in[s])
+            nc.sync.dma_start(scale_window[s][ROW0:P, :].bitcast(I32), scales_in[s].bitcast(I32).rearrange("a q t -> q a t"))
+            nc.vector.memset(scale_window[s][0:ROW0, :].bitcast(I32), 0)
 
         def load_words(s, a):
             nc.sync.dma_start(word_window[s][a][:].bitcast(I32), words_in[s][a].rearrange("p t i -> p (t i)").bitcast(I32))
@@ -86,34 +91,30 @@ def tile_list_clamped_pair_eval_kernel(
             for j in range(PACK):
                 nc.sync.dma_start(we_raw[g][:, j, :], rows[j][:, :, g * 512 : (g + 1) * 512])
 
-        nc.sync.dma_start(offsets[0][:], offs)
-        nc.sync.dma_start(scale_window[0][ROW0:P, :].bitcast(I32), tab_scales.bitcast(I32).rearrange("a q t -> q a t"))
-        nc.vector.memset(scale_window[0][0:ROW0, :].bitcast(I32), 0)
-        nc.sync.dma_start(offsets[1][:], offs2)
-        load_wp(0)
-        for quad in range(4):
-            nc.scalar.dma_start(
-                scale_window[1][32 * quad : 32 * quad + 8, :].bitcast(I32), tab2_scales.bitcast(I32)[:, 4 * quad : 4 * quad + 4, :]
+        def load_wo():
+            nc.sync.dma_start(
+                wo_raw[:].bitcast(I32).rearrange("p (a w) -> p a w", a=PASSES), wo_words.bitcast(I32).rearrange("a p w -> p a w")
             )
-        load_words(0, 0)
-        nc.sync.dma_start(
-            wo_raw[:].bitcast(I32).rearrange("p (a w) -> p a w", a=PASSES), wo_words.bitcast(I32).rearrange("a p w -> p a w")
-        )
-        wo_scale_rows = wo_scales.bitcast(I32).rearrange("a q w -> q a w")
-        for quad in range(4):
-            nc.scalar.dma_start(
-                wo_scale_raw[32 * quad : 32 * quad + 4, :].bitcast(I32).rearrange("p (a w) -> p a w", a=PASSES),
-                wo_scale_rows[4 * quad : 4 * quad + 4],
-            )
-        load_wp(1)
-        load_words(0, 1)
-        load_words(1, 0)
-        load_words(1, 1)
-        cap_rows = cap.rearrange("(q t i o) -> t q i o", t=PACK, i=8, o=1)
-        for t in range(PACK):
-            nc.gpsimd.dma_start(cap_raw[:, t, 0:1], cap_rows[t])
-        load_we(0)
-        load_we(1)
+
+        def load_wo_scales():
+            rows = wo_scales.bitcast(I32).rearrange("a q w -> q a w")
+            for quad in range(4):
+                nc.sync.dma_start(
+                    wo_scale_raw[32 * quad : 32 * quad + 4, :].bitcast(I32).rearrange("p (a w) -> p a w", a=PASSES),
+                    rows[4 * quad : 4 * quad + 4],
+                )
+
+        def load_cap():
+            rows = cap.rearrange("(q t i o) -> t q i o", t=PACK, i=8, o=1)
+            for t in range(PACK):
+                nc.sync.dma_start(cap_raw[:, t, 0:1], rows[t])
+
+        def place_scales(s):
+            for quad in range(4):
+                nc.sync.dma_start(
+                    v_scales[s][32 * quad : 32 * quad + 4, :].bitcast(I32).rearrange("p (a w) -> p a w", a=PASSES),
+                    scale_picked[s][ROW0 + 8 * quad : ROW0 + 8 * quad + 8, :].bitcast(I32),
+                )
 
         def gather_scales(s):
             nc.vector.tensor_copy(scale_picked[s][:], scale_window[s][:].indirect(offsets[s][:]))
@@ -122,10 +123,10 @@ def tile_list_clamped_pair_eval_kernel(
             cols = slice(hf * HALF // 16, (hf + 1) * HALF // 16)
             nc.vector.tensor_copy(v_words[s][a][hf][:], word_window[s][a][:].indirect(offsets[s][:, cols]))
 
-        def round_wp(a):
-            nc.scalar.copy(
-                wp_round[a][:].rearrange("p (t q i j) -> p t q i j", t=PACK, i=8, j=PACK),
-                wp_raw[a][:].rearrange("p j (q t i) -> p t q i j", t=PACK, i=8),
+        def round_wp(copy, a, t0, t1):
+            copy(
+                wp_round[a][:].rearrange("p (t q i j) -> p t q i j", t=PACK, i=8, j=PACK)[:, t0:t1],
+                wp_raw[a][:].rearrange("p j (q t i) -> p t q i j", t=PACK, i=8)[:, t0:t1],
             )
 
         def round_we(g):
@@ -155,10 +156,10 @@ def tile_list_clamped_pair_eval_kernel(
                     if s == 0:
                         lo = a * H + t * P
                         weights, weight_plane = wo_codes[:, 2 * lo : 2 * (lo + P)].bitcast(FP4X4), wo_plane[:, lo : lo + P]
-                        table_plane = v_scales[:, a * S + u * UNIT : a * S + (u + 1) * UNIT]
+                        table_plane = v_scales[s][:, a * S + u * UNIT : a * S + (u + 1) * UNIT]
                     else:
                         weights, weight_plane = wp_codes[a][:, t * P : (t + 1) * P].bitcast(FP8X4), wp_plane[a][:, t * P : (t + 1) * P]
-                        table_plane = scale_picked[1][4 * a : P, u * UNIT : (u + 1) * UNIT]
+                        table_plane = v_scales[s][:, a * S + u * UNIT : a * S + (u + 1) * UNIT]
                     nc.tensor.matmul_mx(
                         out=bank[:, t, :],
                         lhsT=weights,
@@ -198,7 +199,8 @@ def tile_list_clamped_pair_eval_kernel(
             quantise(h_codes[:, cols], h_plane[:, cols], h_round[u][:])
 
         def evaluate(u, g):
-            q, c0 = divmod(u * UNIT, QUARTER)
+            q = max(first for first, count in PIECES if first <= u)
+            c0 = (u - q) * UNIT
             cols = slice(u * UNIT, (u + 1) * UNIT)
             bank = psum.tile([P, PACK, UNIT], F32, name="evaluate_bank")
             for t in range(PACK):
@@ -218,44 +220,61 @@ def tile_list_clamped_pair_eval_kernel(
                     bank[:].rearrange("p t c -> p c t"),
                 )
 
-        def store_y(q, g):
-            rows = out_0[g * 512 : (g + 1) * 512, q * QUARTER : (q + 1) * QUARTER]
-            nc.sync.dma_start(rows.rearrange("(p t) c -> p t c", t=PACK), y_full[q][g][:])
+        def store_y(first, count, g):
+            rows = out_0[g * 512 : (g + 1) * 512, first * UNIT : (first + count) * UNIT]
+            nc.sync.dma_start(rows.rearrange("(p t) c -> p t c", t=PACK), y_full[first][g][:])
 
-        def round_y(q, g):
-            if (q, g) not in SCALAR_ROUNDS:
+        def round_y(first, count, g):
+            if (first, g) not in SCALAR_ROUNDS:
                 nc.vector.tensor_copy(
-                    y_round[q][g][:].rearrange("p (c t) -> p c t", t=PACK), y_full[q][g][:].rearrange("p t c -> p c t")
+                    y_round[first][g][:].rearrange("p (c t) -> p c t", t=PACK), y_full[first][g][:].rearrange("p t c -> p c t")
                 )
 
-        def quantise_y(q, g):
-            cols = slice(q * QUARTER, (q + 1) * QUARTER)
-            quantise(y_codes[g][:, cols], y_plane[:, g * S + q * QUARTER : g * S + (q + 1) * QUARTER], y_round[q][g][:])
-            nc.sync.dma_start(out_1[g].rearrange("p m t -> p (m t)").bitcast(I32)[:, cols], y_codes[g][:, cols].bitcast(I32))
+        def quantise_y(first, count, g):
+            cols = slice(first * UNIT, (first + count) * UNIT)
+            quantise(y_codes[g][:, cols], y_plane[:, g * S + cols.start : g * S + cols.stop], y_round[first][g][:])
+            if first + count in CODE_STORES:
+                done = slice(CODE_STORES[first + count] * UNIT, cols.stop)
+                nc.sync.dma_start(out_1[g].rearrange("p m t -> p (m t)").bitcast(I32)[:, done], y_codes[g][:, done].bitcast(I32))
 
+        load_list_and_scales(0)
+        load_list_and_scales(1)
+        load_words(0, 0)
+        nc.vector.memset(wo_scale_raw[:].bitcast(I32), 0)
+        for s in range(2):
+            nc.vector.memset(v_scales[s][:].bitcast(I32), 0)
+        load_wo_scales()
+        load_wp(0)
         gather_scales(0)
-        for quad in range(4):
-            nc.gpsimd.dma_start(
-                v_scales[32 * quad : 32 * quad + 4, :].bitcast(I32).rearrange("p (a w) -> p a w", a=PASSES),
-                scale_picked[0][ROW0 + 8 * quad : ROW0 + 8 * quad + 8, :].bitcast(I32),
-            )
-        round_wp(0)
+        place_scales(0)
+        load_wo()
+        load_words(0, 1)
         gather_scales(1)
+        place_scales(1)
+        load_words(1, 0)
+        load_cap()
+        load_words(1, 1)
+        load_wp(1)
+        load_we(0)
+        load_we(1)
+        round_wp(nc.scalar.copy, 0, 0, 4)
         gather_words(0, 0, 0)
         gather_words(0, 0, 1)
-        deal_wo()
         quantise(wp_codes[0][:], wp_plane[0][:], wp_round[0][:])
-        round_wp(1)
-        for hf in range(2):
-            gather_words(0, 1, hf)
-            for u in range(4 * hf, 4 * hf + 4):
-                own_side(u)
-        quantise(wp_codes[1][:], wp_plane[1][:], wp_round[1][:])
-        nc.vector.tensor_copy(cap_col[:], cap_raw[:, :, 0])
+        deal_wo()
+        gather_words(0, 1, 0)
+        gather_words(0, 1, 1)
+        for u in range(UNITS):
+            own_side(u)
         gather_words(1, 0, 0)
-        gather_words(1, 1, 0)
         gather_words(1, 0, 1)
+        gather_words(1, 1, 0)
         gather_words(1, 1, 1)
+        nc.vector.tensor_copy(cap_col[:], cap_raw[:, :, 0])
+        round_wp(nc.vector.tensor_copy, 1, 0, 2)
+        round_wp(nc.scalar.copy, 1, 2, 4)
+        for t in (0, 2):
+            quantise(wp_codes[1][:, t * P : (t + 2) * P], wp_plane[1][:, t * P : (t + 2) * P], wp_round[1][:, t * 512 : (t + 2) * 512])
         for g in range(GROUPS):
             round_we(g)
             quantise(we_codes[g][:], we_plane[g][:], we_round[g][:])
@@ -263,19 +282,19 @@ def tile_list_clamped_pair_eval_kernel(
         for step in range(UNITS + 6):
             if step < UNITS:
                 opponent_side(step)
-            if 0 <= step - 1 < UNITS:
-                combine(step - 1)
             if 0 <= step - 2 < UNITS:
                 quantise_h(step - 2)
                 for g in range(GROUPS):
                     evaluate(step - 2, g)
-            if 0 <= step - 3 < UNITS and (step - 3) % 2 == 1:
+            if 0 <= step - 1 < UNITS:
+                combine(step - 1)
+            for first, count in PIECES:
                 for g in range(GROUPS):
-                    store_y((step - 3) // 2, g)
-                    round_y((step - 3) // 2, g)
-            if 0 <= step - 4 < UNITS and (step - 4) % 2 == 1:
-                for g in range(GROUPS):
-                    quantise_y((step - 4) // 2, g)
+                    if step - 3 == first + count - 1:
+                        store_y(first, count, g)
+                        round_y(first, count, g)
+                    if step - 4 == first + count - 1:
+                        quantise_y(first, count, g)
 
         scale_rows = out_2.bitcast(I32).rearrange("g q w -> q g w")
         for quad in range(4):

@@ -1,6 +1,7 @@
 from contextlib import ExitStack
 
 import concourse.mybir as mybir
+from concourse.masks import make_identity
 
 K, T, S, H, N = 1024, 2048, 1024, 512, 1024
 FLOPS = 2 * (2 * K * H * S + H * N * S)
@@ -18,15 +19,22 @@ RELU = mybir.ActivationFunctionType.Relu
 
 P = 128
 PACK = 4
-PASSES = K // (P * PACK)
-GROUPS = N // (P * PACK)
+K_PASS = P * PACK
+PASSES = K // K_PASS
+GROUPS = N // K_PASS
 UNIT = 128
 UNITS = S // UNIT
 HALF = S // 2
-PIECES = ((0, 2), (2, 2), (4, 2), (6, 2))
+PIECE = 2 * UNIT
+PIECES = S // PIECE
+LAG = 0
 ROW0 = 96
-CODE_STORES = {4: 0, 8: 4}
-SCALAR_ROUNDS = ((0, 0), (2, 0), (2, 1))
+REUSED = {}
+UNIT_STORES = ()
+CODE_STORES = {1: 0, 3: 2}
+SCALE_STORES = {3: 0}
+WE_PARTS = 2
+SCALAR_ROUNDS = ((2, 1), (3, 0))
 
 
 def tile_list_clamped_pair_eval_kernel(
@@ -42,111 +50,77 @@ def tile_list_clamped_pair_eval_kernel(
         offsets = [lists.tile([P, S // 16], U16, name=f"offsets{s}") for s in range(2)]
         scale_window = [keep.tile([P, T], U8, name=f"scale_window{s}", align_bytes=64) for s in range(2)]
         scale_picked = [keep.tile([P, S], U8, name=f"scale_picked{s}", align_bytes=64) for s in range(2)]
-        v_scales = [keep.tile([P, PASSES * S], U8, name=f"v_scales{s}", align_bytes=64) for s in range(2)]
+        v_plane = keep.tile([P, PASSES * S], U8, name="v_plane", align_bytes=64)
         word_window = [[keep.tile([P, T], U32, name=f"word_window{s}{a}", align_bytes=64) for a in range(PASSES)] for s in range(2)]
         v_words = [
             [[keep.tile([P, HALF], U32, name=f"v_words{s}{a}{hf}", align_bytes=64) for hf in range(2)] for a in range(PASSES)]
             for s in range(2)
         ]
-        wo_raw = keep.tile([P, PASSES * 2 * H], U8, align_bytes=64)
-        wo_scale_raw = keep.tile([P, PASSES * H], U8, align_bytes=64)
-        wo_codes = keep.tile([P, PASSES * 2 * H], U8, align_bytes=64)
-        wo_plane = keep.tile([P, PASSES * H], U8, align_bytes=64)
+        wo_raw = keep.tile([P, PASSES * 2 * H], U8, name="wo_raw", align_bytes=64)
+        wo_scale_raw = keep.tile([P, PASSES * H], U8, name="wo_scale_raw", align_bytes=64)
+        wo_codes = keep.tile([P, PASSES * 2 * H], U8, name="wo_codes", align_bytes=64)
+        wo_plane = keep.tile([P, PASSES * H], U8, name="wo_plane", align_bytes=64)
         wp_raw = [keep.tile([P, PACK, H], F32, name=f"wp_raw{a}") for a in range(PASSES)]
         wp_round = [keep.tile([P, PACK * H], BF16, name=f"wp_round{a}", align_bytes=64) for a in range(PASSES)]
         wp_codes = [keep.tile([P, H], U32, name=f"wp_codes{a}", align_bytes=64) for a in range(PASSES)]
         wp_plane = [keep.tile([P, H], U8, name=f"wp_plane{a}", align_bytes=64) for a in range(PASSES)]
-        we_raw = [keep.tile([P, PACK, 512], F32, name=f"we_raw{g}") for g in range(GROUPS)]
-        we_round = [keep.tile([P, PACK * 512], BF16, name=f"we_round{g}", align_bytes=64) for g in range(GROUPS)]
-        we_codes = [keep.tile([P, 512], U32, name=f"we_codes{g}", align_bytes=64) for g in range(GROUPS)]
-        we_plane = [keep.tile([P, 512], U8, name=f"we_plane{g}", align_bytes=64) for g in range(GROUPS)]
-        cap_raw = keep.tile([P, PACK, 8], F32)
-        cap_col = keep.tile([P, PACK], F32)
-        own = [keep.tile([P, UNIT * PACK], F32, name=f"own{u}") for u in range(UNITS)]
-        h_codes = keep.tile([P, S], U32, align_bytes=64)
-        h_plane = keep.tile([P, S], U8, align_bytes=64)
-        y_full = {q: [keep.tile([P, PACK, n * UNIT], F32, name=f"y_full{q}{g}") for g in range(GROUPS)] for q, n in PIECES}
-        y_round = {q: [keep.tile([P, n * UNIT * PACK], BF16, name=f"y_round{q}{g}", align_bytes=64) for g in range(GROUPS)] for q, n in PIECES}
+        we_raw = [keep.tile([P, PACK, K_PASS], F32, name=f"we_raw{g}") for g in range(GROUPS)]
+        we_round = {}
+        we_codes = [keep.tile([P, K_PASS], U32, name=f"we_codes{g}", align_bytes=64) for g in range(GROUPS)]
+        we_plane = [keep.tile([P, K_PASS], U8, name=f"we_plane{g}", align_bytes=64) for g in range(GROUPS)]
+        identity = keep.tile([P, P], F32, name="identity")
+        cap_rows = keep.tile([P, P], F32, name="cap_rows")
+        cap_col = keep.tile([P, PACK], F32, name="cap_col")
+        own = [keep.tile([P, UNIT * PACK], F32, name=f"own{u}", tag=f"own{u}", align_bytes=64) for u in range(UNITS)]
+        h_codes = keep.tile([P, S], U32, name="h_codes", align_bytes=64)
+        h_plane = keep.tile([P, S], U8, name="h_plane", align_bytes=64)
+        y_full = [[keep.tile([P, PACK, PIECE], F32, name=f"y_full{q}{g}") for g in range(GROUPS)] for q in range(PIECES)]
+        y_round = [[keep.tile([P, PIECE * PACK], BF16, name=f"y_round{q}{g}", align_bytes=64) for g in range(GROUPS)] for q in range(PIECES)]
         y_codes = [keep.tile([P, S], U32, name=f"y_codes{g}", align_bytes=64) for g in range(GROUPS)]
-        y_plane = keep.tile([P, GROUPS * S], U8, align_bytes=64)
+        y_plane = keep.tile([P, GROUPS * S], U8, name="y_plane", align_bytes=64)
 
         words_in = (tab_words, tab2_words)
-
-        scales_in = (tab_scales, tab2_scales)
-        lists_in = (offs, offs2)
-
-        def load_list_and_scales(s):
-            nc.sync.dma_start(offsets[s][:], lists_in[s])
-            nc.sync.dma_start(scale_window[s][ROW0:P, :].bitcast(I32), scales_in[s].bitcast(I32).rearrange("a q t -> q a t"))
-            nc.vector.memset(scale_window[s][0:ROW0, :].bitcast(I32), 0)
 
         def load_words(s, a):
             nc.sync.dma_start(word_window[s][a][:].bitcast(I32), words_in[s][a].rearrange("p t i -> p (t i)").bitcast(I32))
 
         def load_wp(a):
-            nc.sync.dma_start(wp_raw[a][:], wp[a * 512 : (a + 1) * 512, :].rearrange("(p j) c -> p j c", j=PACK))
+            nc.sync.dma_start(wp_raw[a][:], wp[a * K_PASS : (a + 1) * K_PASS, :].rearrange("(p j) c -> p j c", j=PACK))
 
         def load_we(g):
             rows = we.rearrange("(q j i) n -> j q i n", j=PACK, i=8)
             for j in range(PACK):
-                nc.sync.dma_start(we_raw[g][:, j, :], rows[j][:, :, g * 512 : (g + 1) * 512])
-
-        def load_wo():
-            nc.sync.dma_start(
-                wo_raw[:].bitcast(I32).rearrange("p (a w) -> p a w", a=PASSES), wo_words.bitcast(I32).rearrange("a p w -> p a w")
-            )
-
-        def load_wo_scales():
-            rows = wo_scales.bitcast(I32).rearrange("a q w -> q a w")
-            for quad in range(4):
-                nc.sync.dma_start(
-                    wo_scale_raw[32 * quad : 32 * quad + 4, :].bitcast(I32).rearrange("p (a w) -> p a w", a=PASSES),
-                    rows[4 * quad : 4 * quad + 4],
-                )
-
-        def load_cap():
-            rows = cap.rearrange("(q t i o) -> t q i o", t=PACK, i=8, o=1)
-            for t in range(PACK):
-                nc.sync.dma_start(cap_raw[:, t, 0:1], rows[t])
-
-        def place_scales(s):
-            for quad in range(4):
-                nc.sync.dma_start(
-                    v_scales[s][32 * quad : 32 * quad + 4, :].bitcast(I32).rearrange("p (a w) -> p a w", a=PASSES),
-                    scale_picked[s][ROW0 + 8 * quad : ROW0 + 8 * quad + 8, :].bitcast(I32),
-                )
+                nc.sync.dma_start(we_raw[g][:, j, :], rows[j][:, :, g * K_PASS : (g + 1) * K_PASS])
 
         def gather_scales(s):
             nc.vector.tensor_copy(scale_picked[s][:], scale_window[s][:].indirect(offsets[s][:]))
 
-        def gather_words(s, a, hf):
-            cols = slice(hf * HALF // 16, (hf + 1) * HALF // 16)
-            nc.vector.tensor_copy(v_words[s][a][hf][:], word_window[s][a][:].indirect(offsets[s][:, cols]))
+        def gather_words(s, a):
+            for hf in range(2):
+                cols = slice(hf * HALF // 16, (hf + 1) * HALF // 16)
+                nc.vector.tensor_copy(v_words[s][a][hf][:], word_window[s][a][:].indirect(offsets[s][:, cols]))
 
-        def round_wp(copy, a, t0, t1):
+        def round_wp(copy, a, t):
             copy(
-                wp_round[a][:].rearrange("p (t q i j) -> p t q i j", t=PACK, i=8, j=PACK)[:, t0:t1],
-                wp_raw[a][:].rearrange("p j (q t i) -> p t q i j", t=PACK, i=8)[:, t0:t1],
+                wp_round[a][:].rearrange("p (t q h i j) -> p t q h j i", t=PACK, h=2, i=4, j=PACK)[:, t],
+                wp_raw[a][:].rearrange("p j (q t h i) -> p t q h j i", t=PACK, h=2, i=4)[:, t],
             )
 
-        def round_we(g):
-            nc.scalar.copy(
-                we_round[g][:].rearrange("p (t m j) -> p m t j", t=PACK, j=PACK),
-                we_raw[g][:].rearrange("p j (m t) -> p m t j", t=PACK),
+        def round_we(copy, g, part):
+            ts = slice(2 * part, 2 * part + 2)
+            tag = REUSED.get((g, part), f"we_round{g}{part}")
+            we_round[g, part] = keep.tile([P, 2 * K_PASS], BF16, name=f"we_round{g}{part}", tag=tag, align_bytes=64)
+            copy(
+                we_round[g, part][:].rearrange("p (t m j) -> p m j t", t=2, j=PACK),
+                we_raw[g][:].rearrange("p j (m t) -> p m j t", t=PACK)[:, :, :, ts],
             )
+
+        def quantise_we(g, part):
+            cols = slice(2 * part * P, (2 * part + 2) * P)
+            quantise(we_codes[g][:, cols], we_plane[g][:, cols], we_round[g, part][:])
 
         def quantise(codes, plane, values):
             nc.vector.quantize_mx(out=codes.bitcast(FP8X4), scales=plane, in_=values)
-
-        def deal_wo():
-            nc.vector.tensor_copy(
-                wo_codes[:].bitcast(I32).rearrange("p (a t q w) -> p a t q w", a=PASSES, t=PACK, w=4),
-                wo_raw[:].bitcast(I32).rearrange("p (a q t w) -> p a t q w", a=PASSES, t=PACK, w=4),
-            )
-            nc.vector.tensor_copy(
-                wo_plane[:].bitcast(I32).rearrange("p (a t q w) -> p a t q w", a=PASSES, t=PACK, w=2),
-                wo_scale_raw[:].bitcast(I32).rearrange("p (a q t w) -> p a t q w", a=PASSES, t=PACK, w=2),
-            )
 
         def project(s, u):
             bank = psum.tile([P, PACK, UNIT], F32, name="project_bank")
@@ -156,10 +130,10 @@ def tile_list_clamped_pair_eval_kernel(
                     if s == 0:
                         lo = a * H + t * P
                         weights, weight_plane = wo_codes[:, 2 * lo : 2 * (lo + P)].bitcast(FP4X4), wo_plane[:, lo : lo + P]
-                        table_plane = v_scales[s][:, a * S + u * UNIT : a * S + (u + 1) * UNIT]
+                        table_plane = v_plane[:, a * S + u * UNIT : a * S + (u + 1) * UNIT]
                     else:
                         weights, weight_plane = wp_codes[a][:, t * P : (t + 1) * P].bitcast(FP8X4), wp_plane[a][:, t * P : (t + 1) * P]
-                        table_plane = v_scales[s][:, a * S + u * UNIT : a * S + (u + 1) * UNIT]
+                        table_plane = scale_picked[1][4 * a : P, u * UNIT : (u + 1) * UNIT]
                     nc.tensor.matmul_mx(
                         out=bank[:, t, :],
                         lhsT=weights,
@@ -199,8 +173,7 @@ def tile_list_clamped_pair_eval_kernel(
             quantise(h_codes[:, cols], h_plane[:, cols], h_round[u][:])
 
         def evaluate(u, g):
-            q = max(first for first, count in PIECES if first <= u)
-            c0 = (u - q) * UNIT
+            q, c0 = divmod(u * UNIT, PIECE)
             cols = slice(u * UNIT, (u + 1) * UNIT)
             bank = psum.tile([P, PACK, UNIT], F32, name="evaluate_bank")
             for t in range(PACK):
@@ -214,92 +187,134 @@ def tile_list_clamped_pair_eval_kernel(
                     stop=True,
                 )
             nc.scalar.copy(y_full[q][g][:, :, c0 : c0 + UNIT], bank[:])
-            if (q, g) in SCALAR_ROUNDS:
-                nc.scalar.copy(
-                    y_round[q][g][:, PACK * c0 : PACK * (c0 + UNIT)].rearrange("p (c t) -> p c t", t=PACK),
-                    bank[:].rearrange("p t c -> p c t"),
-                )
+            width = UNIT if (q, g) in UNIT_STORES else PIECE
+            if (c0 + UNIT) % width == 0:
+                rows = out_0[g * K_PASS : (g + 1) * K_PASS, cols.stop - width : cols.stop]
+                nc.sync.dma_start(rows.rearrange("(p t) c -> p t c", t=PACK), y_full[q][g][:, :, c0 + UNIT - width : c0 + UNIT])
 
-        def store_y(first, count, g):
-            rows = out_0[g * 512 : (g + 1) * 512, first * UNIT : (first + count) * UNIT]
-            nc.sync.dma_start(rows.rearrange("(p t) c -> p t c", t=PACK), y_full[first][g][:])
+        def round_y(q, g):
+            copy = nc.scalar.copy if (q, g) in SCALAR_ROUNDS else nc.vector.tensor_copy
+            copy(
+                y_round[q][g][:].rearrange("p (c i t) -> p c t i", t=PACK, i=4),
+                y_full[q][g][:].rearrange("p t (c i) -> p c t i", i=4),
+            )
 
-        def round_y(first, count, g):
-            if (first, g) not in SCALAR_ROUNDS:
-                nc.vector.tensor_copy(
-                    y_round[first][g][:].rearrange("p (c t) -> p c t", t=PACK), y_full[first][g][:].rearrange("p t c -> p c t")
-                )
-
-        def quantise_y(first, count, g):
-            cols = slice(first * UNIT, (first + count) * UNIT)
-            quantise(y_codes[g][:, cols], y_plane[:, g * S + cols.start : g * S + cols.stop], y_round[first][g][:])
-            if first + count in CODE_STORES:
-                done = slice(CODE_STORES[first + count] * UNIT, cols.stop)
+        def quantise_y(q, g):
+            cols = slice(q * PIECE, (q + 1) * PIECE)
+            quantise(y_codes[g][:, cols], y_plane[:, g * S + cols.start : g * S + cols.stop], y_round[q][g][:])
+            if q in CODE_STORES:
+                done = slice(CODE_STORES[q] * PIECE, cols.stop)
                 nc.sync.dma_start(out_1[g].rearrange("p m t -> p (m t)").bitcast(I32)[:, done], y_codes[g][:, done].bitcast(I32))
+            if q in SCALE_STORES and g == GROUPS - 1:
+                words = slice(SCALE_STORES[q] * PIECE // 4, cols.stop // 4)
+                rows = out_2.bitcast(I32).rearrange("g (quad r) w -> r quad g w", r=4)
+                for r in range(4):
+                    queue = nc.scalar if q == PIECES - 1 and r % 2 == 1 else nc.sync
+                    queue.dma_start(rows[r][:, :, words], y_plane[r:P:32, :].bitcast(I32).rearrange("p (g w) -> p g w", g=GROUPS)[:, :, words])
 
-        load_list_and_scales(0)
-        load_list_and_scales(1)
-        load_words(0, 0)
+        def load_tab2_scales():
+            for quad in range(4):
+                nc.sync.dma_start(
+                    scale_window[1][32 * quad : 32 * quad + 8, :].bitcast(I32), tab2_scales.bitcast(I32)[:, 4 * quad : 4 * quad + 4, :]
+                )
+
+        def load_wo_scales():
+            rows = wo_scales.bitcast(I32).rearrange("a (quad r) w -> r quad a w", r=4)
+            for r in range(4):
+                nc.sync.dma_start(wo_scale_raw[r:P:32, :].bitcast(I32).rearrange("p (a w) -> p a w", a=PASSES), rows[r])
+
+        def load_cap():
+            nc.sync.dma_start(cap_rows[0:PACK, :].rearrange("t (q i) -> t q i", i=8), cap.rearrange("(q t i) -> t q i", t=PACK, i=8))
+
+        def load_wo():
+            nc.sync.dma_start(
+                wo_raw[:].bitcast(I32).rearrange("p (a w) -> p a w", a=PASSES), wo_words.bitcast(I32).rearrange("a p w -> p a w")
+            )
+
+        def place_scales():
+            for r in range(4):
+                nc.sync.dma_start(
+                    v_plane[r:P:32, :].bitcast(I32).rearrange("p (a w) -> p a w", a=PASSES),
+                    scale_picked[0][ROW0 + 8 * r : ROW0 + 8 * r + 8, :].bitcast(I32),
+                )
+
+        def deal_wo():
+            for dealt, raw, run in ((wo_plane, wo_scale_raw, 2), (wo_codes, wo_raw, 4)):
+                nc.vector.tensor_copy(
+                    dealt[:].bitcast(I32).rearrange("p (a t q w) -> p a t q w", a=PASSES, t=PACK, w=run),
+                    raw[:].bitcast(I32).rearrange("p (a q t w) -> p a t q w", a=PASSES, t=PACK, w=run),
+                )
+
+        nc.vector.memset(scale_window[1][:].bitcast(I32), 0)
         nc.vector.memset(wo_scale_raw[:].bitcast(I32), 0)
-        for s in range(2):
-            nc.vector.memset(v_scales[s][:].bitcast(I32), 0)
+        nc.vector.memset(scale_window[0][0:ROW0, :].bitcast(I32), 0)
+        nc.vector.memset(v_plane[:].bitcast(I32), 0)
+        nc.vector.memset(cap_rows[:], 0.0)
+        make_identity(nc, identity[:])
+
+        nc.sync.dma_start(offsets[0][:], offs)
+        for a in range(PASSES):
+            nc.sync.dma_start(
+                scale_window[0][ROW0 + a : P : 2, :].bitcast(I32), tab_scales[a].bitcast(I32).rearrange("(quad r) w -> r quad w", r=4)
+            )
+        nc.sync.dma_start(offsets[1][:], offs2)
+        load_tab2_scales()
+        load_words(0, 0)
         load_wo_scales()
+        load_cap()
         load_wp(0)
         gather_scales(0)
-        place_scales(0)
+        place_scales()
         load_wo()
         load_words(0, 1)
-        gather_scales(1)
-        place_scales(1)
         load_words(1, 0)
-        load_cap()
         load_words(1, 1)
         load_wp(1)
         load_we(0)
         load_we(1)
-        round_wp(nc.scalar.copy, 0, 0, 4)
-        gather_words(0, 0, 0)
-        gather_words(0, 0, 1)
+
+        gather_scales(1)
+        cap_bank = psum.tile([P, P], F32, name="project_bank")
+        nc.tensor.transpose(cap_bank[:], cap_rows[:], identity[:])
+        nc.scalar.copy(cap_col[:], cap_bank[:, 0:PACK])
+        for t in range(PACK):
+            round_wp(nc.scalar.copy, 0, t)
+        gather_words(0, 0)
         quantise(wp_codes[0][:], wp_plane[0][:], wp_round[0][:])
         deal_wo()
-        gather_words(0, 1, 0)
-        gather_words(0, 1, 1)
+        gather_words(0, 1)
         for u in range(UNITS):
             own_side(u)
-        gather_words(1, 0, 0)
-        gather_words(1, 0, 1)
-        gather_words(1, 1, 0)
-        gather_words(1, 1, 1)
-        nc.vector.tensor_copy(cap_col[:], cap_raw[:, :, 0])
-        round_wp(nc.vector.tensor_copy, 1, 0, 2)
-        round_wp(nc.scalar.copy, 1, 2, 4)
+        gather_words(1, 0)
+        gather_words(1, 1)
+        for t in range(PACK):
+            round_wp(nc.vector.tensor_copy if t < 2 else nc.scalar.copy, 1, t)
         for t in (0, 2):
-            quantise(wp_codes[1][:, t * P : (t + 2) * P], wp_plane[1][:, t * P : (t + 2) * P], wp_round[1][:, t * 512 : (t + 2) * 512])
-        for g in range(GROUPS):
-            round_we(g)
-            quantise(we_codes[g][:], we_plane[g][:], we_round[g][:])
+            quantise(wp_codes[1][:, t * P : (t + 2) * P], wp_plane[1][:, t * P : (t + 2) * P], wp_round[1][:, t * K_PASS : (t + 2) * K_PASS])
+        for part in range(WE_PARTS):
+            round_we(nc.vector.tensor_copy if part < 0 else nc.scalar.copy, 0, part)
+        for part in range(WE_PARTS):
+            quantise_we(0, part)
 
-        for step in range(UNITS + 6):
+        for step in range(UNITS + 2 + LAG):
             if step < UNITS:
                 opponent_side(step)
             if 0 <= step - 2 < UNITS:
                 quantise_h(step - 2)
-                for g in range(GROUPS):
-                    evaluate(step - 2, g)
+                evaluate(step - 2, 0)
+            if step == 1 + LAG:
+                for part in range(WE_PARTS):
+                    round_we(nc.vector.tensor_copy if part < 0 else nc.scalar.copy, 1, part)
+                for part in range(WE_PARTS):
+                    quantise_we(1, part)
+            if 0 <= step - 2 - LAG:
+                evaluate(step - 2 - LAG, 1)
             if 0 <= step - 1 < UNITS:
                 combine(step - 1)
-            for first, count in PIECES:
-                for g in range(GROUPS):
-                    if step - 3 == first + count - 1:
-                        store_y(first, count, g)
-                        round_y(first, count, g)
-                    if step - 4 == first + count - 1:
-                        quantise_y(first, count, g)
 
-        scale_rows = out_2.bitcast(I32).rearrange("g q w -> q g w")
-        for quad in range(4):
-            queue = nc.sync if quad % 2 == 0 else nc.scalar
-            queue.dma_start(
-                scale_rows[4 * quad : 4 * quad + 4],
-                y_plane[32 * quad : 32 * quad + 4, :].bitcast(I32).rearrange("p (g w) -> p g w", g=GROUPS),
-            )
+        blocks = [(q, g) for q in range(PIECES) for g in range(GROUPS)]
+        for step in range(len(blocks) + 1):
+            if step < len(blocks):
+                round_y(*blocks[step])
+            if step > 0:
+                quantise_y(*blocks[step - 1])

@@ -22,19 +22,20 @@ PACK = 4
 K_PASS = P * PACK
 PASSES = K // K_PASS
 GROUPS = N // K_PASS
-UNIT = 128
-UNITS = S // UNIT
 HALF = S // 2
-PIECE = 2 * UNIT
-PIECES = S // PIECE
-LAG = 0
+BANK = 512
 ROW0 = 96
-REUSED = {}
-UNIT_STORES = ()
+WIDTHS = (512, 512)
+STARTS = [sum(WIDTHS[:q]) for q in range(len(WIDTHS))]
+PIECES = len(WIDTHS)
+BLOCK = 256
+STORE_SLOTS = 1
 CODE_STORES = {1: 0, 3: 2}
 SCALE_STORES = {3: 0}
-WE_PARTS = 2
-SCALAR_ROUNDS = ((2, 1), (3, 0))
+SCALAR_ROUNDS = ((2, 1),)
+WP_VECTOR = (4, 4)
+WE_VECTOR = ()
+OWN_VECTOR = ()
 
 
 def tile_list_clamped_pair_eval_kernel(
@@ -44,7 +45,6 @@ def tile_list_clamped_pair_eval_kernel(
     with ExitStack() as ctx:
         lists = ctx.enter_context(tc.tile_pool(name="lists", bufs=1))
         keep = ctx.enter_context(tc.tile_pool(name="keep", bufs=1))
-        ring = ctx.enter_context(tc.tile_pool(name="ring", bufs=3))
         psum = ctx.enter_context(tc.psum_pool(name="psum", bufs=4))
 
         offsets = [lists.tile([P, S // 16], U16, name=f"offsets{s}") for s in range(2)]
@@ -52,10 +52,7 @@ def tile_list_clamped_pair_eval_kernel(
         scale_picked = [keep.tile([P, S], U8, name=f"scale_picked{s}", align_bytes=64) for s in range(2)]
         v_plane = keep.tile([P, PASSES * S], U8, name="v_plane", align_bytes=64)
         word_window = [[keep.tile([P, T], U32, name=f"word_window{s}{a}", align_bytes=64) for a in range(PASSES)] for s in range(2)]
-        v_words = [
-            [[keep.tile([P, HALF], U32, name=f"v_words{s}{a}{hf}", align_bytes=64) for hf in range(2)] for a in range(PASSES)]
-            for s in range(2)
-        ]
+        v_words = [[keep.tile([P, S], U32, name=f"v_words{s}{a}", align_bytes=64) for a in range(PASSES)] for s in range(2)]
         wo_raw = keep.tile([P, PASSES * 2 * H], U8, name="wo_raw", align_bytes=64)
         wo_scale_raw = keep.tile([P, PASSES * H], U8, name="wo_scale_raw", align_bytes=64)
         wo_codes = keep.tile([P, PASSES * 2 * H], U8, name="wo_codes", align_bytes=64)
@@ -65,17 +62,19 @@ def tile_list_clamped_pair_eval_kernel(
         wp_codes = [keep.tile([P, H], U32, name=f"wp_codes{a}", align_bytes=64) for a in range(PASSES)]
         wp_plane = [keep.tile([P, H], U8, name=f"wp_plane{a}", align_bytes=64) for a in range(PASSES)]
         we_raw = [keep.tile([P, PACK, K_PASS], F32, name=f"we_raw{g}") for g in range(GROUPS)]
-        we_round = {}
+        we_round = [[keep.tile([P, 2 * K_PASS], BF16, name=f"we_round{g}{part}", align_bytes=64) for part in range(2)] for g in range(GROUPS)]
         we_codes = [keep.tile([P, K_PASS], U32, name=f"we_codes{g}", align_bytes=64) for g in range(GROUPS)]
         we_plane = [keep.tile([P, K_PASS], U8, name=f"we_plane{g}", align_bytes=64) for g in range(GROUPS)]
         identity = keep.tile([P, P], F32, name="identity")
         cap_rows = keep.tile([P, P], F32, name="cap_rows")
         cap_col = keep.tile([P, PACK], F32, name="cap_col")
-        own = [keep.tile([P, UNIT * PACK], F32, name=f"own{u}", tag=f"own{u}", align_bytes=64) for u in range(UNITS)]
+        own = [keep.tile([P, PACK, HALF], F32, name=f"own{hf}") for hf in range(2)]
+        product = [keep.tile([P, PACK, HALF], F32, name=f"product{hf}", tag="product") for hf in range(2)]
+        h_round = [keep.tile([P, PACK * BLOCK], BF16, name=f"h_round{b}", align_bytes=64) for b in range(S // BLOCK)]
         h_codes = keep.tile([P, S], U32, name="h_codes", align_bytes=64)
         h_plane = keep.tile([P, S], U8, name="h_plane", align_bytes=64)
-        y_full = [[keep.tile([P, PACK, PIECE], F32, name=f"y_full{q}{g}") for g in range(GROUPS)] for q in range(PIECES)]
-        y_round = [[keep.tile([P, PIECE * PACK], BF16, name=f"y_round{q}{g}", align_bytes=64) for g in range(GROUPS)] for q in range(PIECES)]
+        y_full = [[keep.tile([P, PACK, HALF], F32, name=f"y_full{hf}{g}") for g in range(GROUPS)] for hf in range(2)]
+        y_round = [[keep.tile([P, PACK * BLOCK], BF16, name=f"y_round{b}{g}", align_bytes=64) for g in range(GROUPS)] for b in range(S // BLOCK)]
         y_codes = [keep.tile([P, S], U32, name=f"y_codes{g}", align_bytes=64) for g in range(GROUPS)]
         y_plane = keep.tile([P, GROUPS * S], U8, name="y_plane", align_bytes=64)
 
@@ -98,7 +97,7 @@ def tile_list_clamped_pair_eval_kernel(
         def gather_words(s, a):
             for hf in range(2):
                 cols = slice(hf * HALF // 16, (hf + 1) * HALF // 16)
-                nc.vector.tensor_copy(v_words[s][a][hf][:], word_window[s][a][:].indirect(offsets[s][:, cols]))
+                nc.vector.tensor_copy(v_words[s][a][:, hf * HALF : (hf + 1) * HALF], word_window[s][a][:].indirect(offsets[s][:, cols]))
 
         def round_wp(copy, a, t):
             copy(
@@ -108,109 +107,127 @@ def tile_list_clamped_pair_eval_kernel(
 
         def round_we(copy, g, part):
             ts = slice(2 * part, 2 * part + 2)
-            tag = REUSED.get((g, part), f"we_round{g}{part}")
-            we_round[g, part] = keep.tile([P, 2 * K_PASS], BF16, name=f"we_round{g}{part}", tag=tag, align_bytes=64)
             copy(
-                we_round[g, part][:].rearrange("p (t m j) -> p m j t", t=2, j=PACK),
+                we_round[g][part][:].rearrange("p (t m j) -> p m j t", t=2, j=PACK),
                 we_raw[g][:].rearrange("p j (m t) -> p m j t", t=PACK)[:, :, :, ts],
             )
 
         def quantise_we(g, part):
             cols = slice(2 * part * P, (2 * part + 2) * P)
-            quantise(we_codes[g][:, cols], we_plane[g][:, cols], we_round[g, part][:])
+            quantise(we_codes[g][:, cols], we_plane[g][:, cols], we_round[g][part][:])
 
         def quantise(codes, plane, values):
             nc.vector.quantize_mx(out=codes.bitcast(FP8X4), scales=plane, in_=values)
 
-        def project(s, u):
-            bank = psum.tile([P, PACK, UNIT], F32, name="project_bank")
-            hf, c0 = divmod(u * UNIT, HALF)
+        def own_side(hf):
+            cols = slice(hf * HALF, (hf + 1) * HALF)
             for t in range(PACK):
+                bank = psum.tile([P, BANK], F32, name="project_bank")
                 for a in range(PASSES):
-                    if s == 0:
-                        lo = a * H + t * P
-                        weights, weight_plane = wo_codes[:, 2 * lo : 2 * (lo + P)].bitcast(FP4X4), wo_plane[:, lo : lo + P]
-                        table_plane = v_plane[:, a * S + u * UNIT : a * S + (u + 1) * UNIT]
-                    else:
-                        weights, weight_plane = wp_codes[a][:, t * P : (t + 1) * P].bitcast(FP8X4), wp_plane[a][:, t * P : (t + 1) * P]
-                        table_plane = scale_picked[1][4 * a : P, u * UNIT : (u + 1) * UNIT]
+                    lo = a * H + t * P
                     nc.tensor.matmul_mx(
-                        out=bank[:, t, :],
-                        lhsT=weights,
-                        lhsT_scale=weight_plane,
-                        rhs=v_words[s][a][hf][:, c0 : c0 + UNIT].bitcast(FP8X4),
-                        rhs_scale=table_plane,
+                        out=bank[:],
+                        lhsT=wo_codes[:, 2 * lo : 2 * (lo + P)].bitcast(FP4X4),
+                        lhsT_scale=wo_plane[:, lo : lo + P],
+                        rhs=v_words[0][a][:, cols].bitcast(FP8X4),
+                        rhs_scale=v_plane[:, a * S + cols.start : a * S + cols.stop],
                         start=(a == 0),
                         stop=(a == PASSES - 1),
                     )
-            return bank
+                if (hf, t) in OWN_VECTOR:
+                    nc.vector.tensor_scalar(out=own[hf][:, t, :], in0=bank[:], scalar1=0.0, scalar2=1.0, op0=ALU.max, op1=ALU.min)
+                else:
+                    nc.scalar.activation(own[hf][:, t, :], bank[:], RELU, bias=1.0, scale=-1.0)
+            first = len([t for t in range(PACK) if (hf, t) in OWN_VECTOR])
+            if first < PACK:
+                nc.scalar.activation(own[hf][:, first:PACK, :], own[hf][:, first:PACK, :], RELU, bias=1.0, scale=-1.0)
 
-        def own_side(u):
-            bank = project(0, u)
-            nc.scalar.activation(own[u][:].rearrange("p (c t) -> p c t", t=PACK), bank[:].rearrange("p t c -> p c t"), RELU)
+        def multiply(start, width):
+            cols = slice(start, start + width)
+            hf, c0 = divmod(start, HALF)
+            slots = BANK // width
+            for t0 in range(0, PACK, slots):
+                bank = psum.tile([P, slots, width], F32, name="project_bank")
+                for e in range(slots):
+                    t = t0 + e
+                    for a in range(PASSES):
+                        nc.tensor.matmul_mx(
+                            out=bank[:, e, :],
+                            lhsT=wp_codes[a][:, t * P : (t + 1) * P].bitcast(FP8X4),
+                            lhsT_scale=wp_plane[a][:, t * P : (t + 1) * P],
+                            rhs=v_words[1][a][:, cols].bitcast(FP8X4),
+                            rhs_scale=scale_picked[1][4 * a : P, cols],
+                            start=(a == 0),
+                            stop=(a == PASSES - 1),
+                        )
+                for e in range(slots):
+                    t = t0 + e
+                    nc.vector.scalar_tensor_tensor(
+                        out=product[hf][:, t, c0 : c0 + width],
+                        in0=bank[:, e, :],
+                        scalar=cap_col[:, t : t + 1],
+                        in1=own[hf][:, t, c0 : c0 + width],
+                        op0=ALU.min,
+                        op1=ALU.mult,
+                    )
 
-        opp = {}
-        h_round = {}
-
-        def opponent_side(u):
-            bank = project(1, u)
-            opp[u] = ring.tile([P, UNIT * PACK], F32, name="opp")
-            nc.vector.scalar_tensor_tensor(
-                out=opp[u][:].rearrange("p (c t) -> p c t", t=PACK),
-                in0=bank[:].rearrange("p t c -> p c t"),
-                scalar=0.0,
-                in1=cap_col[:].unsqueeze(1).to_broadcast([P, UNIT, PACK]),
+        def round_h(b):
+            hf, c0 = divmod(b * BLOCK, HALF)
+            nc.vector.tensor_scalar(
+                out=h_round[b][:].rearrange("p (c i t) -> p c t i", t=PACK, i=4),
+                in0=product[hf][:, :, c0 : c0 + BLOCK].rearrange("p t (c i) -> p c t i", i=4),
+                scalar1=0.0,
+                scalar2=None,
                 op0=ALU.max,
-                op1=ALU.min,
             )
 
-        def combine(u):
-            h_round[u] = ring.tile([P, UNIT * PACK], BF16, name="h_round", align_bytes=64)
-            nc.vector.scalar_tensor_tensor(out=h_round[u][:], in0=own[u][:], scalar=1.0, in1=opp[u][:], op0=ALU.min, op1=ALU.mult)
+        def quantise_h(b):
+            cols = slice(b * BLOCK, (b + 1) * BLOCK)
+            quantise(h_codes[:, cols], h_plane[:, cols], h_round[b][:])
 
-        def quantise_h(u):
-            cols = slice(u * UNIT, (u + 1) * UNIT)
-            quantise(h_codes[:, cols], h_plane[:, cols], h_round[u][:])
+        def evaluate(g, start, width):
+            cols = slice(start, start + width)
+            hf, c0 = divmod(start, HALF)
+            slots = BANK // width
+            rows = out_0[g * K_PASS : (g + 1) * K_PASS, cols].rearrange("(p t) c -> p t c", t=PACK)
+            for t0 in range(0, PACK, slots):
+                bank = psum.tile([P, slots, width], F32, name="evaluate_bank")
+                for e in range(slots):
+                    t = t0 + e
+                    nc.tensor.matmul_mx(
+                        out=bank[:, e, :],
+                        lhsT=we_codes[g][:, t * P : (t + 1) * P].bitcast(FP8X4),
+                        lhsT_scale=we_plane[g][:, t * P : (t + 1) * P],
+                        rhs=h_codes[:, cols].bitcast(FP8X4),
+                        rhs_scale=h_plane[:, cols],
+                        start=True,
+                        stop=True,
+                    )
+                result = y_full[hf][g][:, t0 : t0 + slots, c0 : c0 + width]
+                nc.scalar.copy(result, bank[:])
+                nc.sync.dma_start(rows[:, t0 : t0 + slots, :], result)
 
-        def evaluate(u, g):
-            q, c0 = divmod(u * UNIT, PIECE)
-            cols = slice(u * UNIT, (u + 1) * UNIT)
-            bank = psum.tile([P, PACK, UNIT], F32, name="evaluate_bank")
-            for t in range(PACK):
-                nc.tensor.matmul_mx(
-                    out=bank[:, t, :],
-                    lhsT=we_codes[g][:, t * P : (t + 1) * P].bitcast(FP8X4),
-                    lhsT_scale=we_plane[g][:, t * P : (t + 1) * P],
-                    rhs=h_codes[:, cols].bitcast(FP8X4),
-                    rhs_scale=h_plane[:, cols],
-                    start=True,
-                    stop=True,
-                )
-            nc.scalar.copy(y_full[q][g][:, :, c0 : c0 + UNIT], bank[:])
-            width = UNIT if (q, g) in UNIT_STORES else PIECE
-            if (c0 + UNIT) % width == 0:
-                rows = out_0[g * K_PASS : (g + 1) * K_PASS, cols.stop - width : cols.stop]
-                nc.sync.dma_start(rows.rearrange("(p t) c -> p t c", t=PACK), y_full[q][g][:, :, c0 + UNIT - width : c0 + UNIT])
-
-        def round_y(q, g):
-            copy = nc.scalar.copy if (q, g) in SCALAR_ROUNDS else nc.vector.tensor_copy
+        def round_y(b, g):
+            hf, c0 = divmod(b * BLOCK, HALF)
+            copy = nc.scalar.copy if (b, g) in SCALAR_ROUNDS else nc.vector.tensor_copy
             copy(
-                y_round[q][g][:].rearrange("p (c i t) -> p c t i", t=PACK, i=4),
-                y_full[q][g][:].rearrange("p t (c i) -> p c t i", i=4),
+                y_round[b][g][:].rearrange("p (c i t) -> p c t i", t=PACK, i=4),
+                y_full[hf][g][:, :, c0 : c0 + BLOCK].rearrange("p t (c i) -> p c t i", i=4),
             )
 
-        def quantise_y(q, g):
-            cols = slice(q * PIECE, (q + 1) * PIECE)
-            quantise(y_codes[g][:, cols], y_plane[:, g * S + cols.start : g * S + cols.stop], y_round[q][g][:])
-            if q in CODE_STORES:
-                done = slice(CODE_STORES[q] * PIECE, cols.stop)
-                nc.sync.dma_start(out_1[g].rearrange("p m t -> p (m t)").bitcast(I32)[:, done], y_codes[g][:, done].bitcast(I32))
-            if q in SCALE_STORES and g == GROUPS - 1:
-                words = slice(SCALE_STORES[q] * PIECE // 4, cols.stop // 4)
-                rows = out_2.bitcast(I32).rearrange("g (quad r) w -> r quad g w", r=4)
-                for r in range(4):
-                    queue = nc.scalar if q == PIECES - 1 and r % 2 == 1 else nc.sync
-                    queue.dma_start(rows[r][:, :, words], y_plane[r:P:32, :].bitcast(I32).rearrange("p (g w) -> p g w", g=GROUPS)[:, :, words])
+        def quantise_y(b, g):
+            cols = slice(b * BLOCK, (b + 1) * BLOCK)
+            quantise(y_codes[g][:, cols], y_plane[:, g * S + cols.start : g * S + cols.stop], y_round[b][g][:])
+
+        def store_codes(g, first, last):
+            done = slice(first * BLOCK, last * BLOCK)
+            nc.sync.dma_start(out_1[g].rearrange("p m t -> p (m t)").bitcast(I32)[:, done], y_codes[g][:, done].bitcast(I32))
+
+        def store_scales():
+            rows = out_2.bitcast(I32).rearrange("g (quad r) w -> r quad g w", r=4)
+            for r in range(4):
+                queue = nc.scalar if r % 2 == 1 else nc.sync
+                queue.dma_start(rows[r], y_plane[r:P:32, :].bitcast(I32).rearrange("p (g w) -> p g w", g=GROUPS))
 
         def load_tab2_scales():
             for quad in range(4):
@@ -262,14 +279,14 @@ def tile_list_clamped_pair_eval_kernel(
         load_words(0, 0)
         load_wo_scales()
         load_cap()
-        load_wp(0)
-        gather_scales(0)
-        place_scales()
         load_wo()
         load_words(0, 1)
+        gather_scales(0)
+        place_scales()
+        load_wp(0)
         load_words(1, 0)
-        load_words(1, 1)
         load_wp(1)
+        load_words(1, 1)
         load_we(0)
         load_we(1)
 
@@ -277,44 +294,58 @@ def tile_list_clamped_pair_eval_kernel(
         cap_bank = psum.tile([P, P], F32, name="project_bank")
         nc.tensor.transpose(cap_bank[:], cap_rows[:], identity[:])
         nc.scalar.copy(cap_col[:], cap_bank[:, 0:PACK])
-        for t in range(PACK):
-            round_wp(nc.scalar.copy, 0, t)
         gather_words(0, 0)
-        quantise(wp_codes[0][:], wp_plane[0][:], wp_round[0][:])
         deal_wo()
         gather_words(0, 1)
-        for u in range(UNITS):
-            own_side(u)
-        gather_words(1, 0)
-        gather_words(1, 1)
-        for t in range(PACK):
-            round_wp(nc.vector.tensor_copy if t < 2 else nc.scalar.copy, 1, t)
-        for t in (0, 2):
-            quantise(wp_codes[1][:, t * P : (t + 2) * P], wp_plane[1][:, t * P : (t + 2) * P], wp_round[1][:, t * K_PASS : (t + 2) * K_PASS])
-        for part in range(WE_PARTS):
-            round_we(nc.vector.tensor_copy if part < 0 else nc.scalar.copy, 0, part)
-        for part in range(WE_PARTS):
-            quantise_we(0, part)
+        for hf in range(2):
+            own_side(hf)
+        for a in range(PASSES):
+            for t in range(PACK):
+                round_wp(nc.vector.tensor_copy if t < WP_VECTOR[a] else nc.scalar.copy, a, t)
+            for t in (0, 2):
+                quantise(wp_codes[a][:, t * P : (t + 2) * P], wp_plane[a][:, t * P : (t + 2) * P], wp_round[a][:, t * K_PASS : (t + 2) * K_PASS])
+            gather_words(1, a)
 
-        for step in range(UNITS + 2 + LAG):
-            if step < UNITS:
-                opponent_side(step)
-            if 0 <= step - 2 < UNITS:
-                quantise_h(step - 2)
-                evaluate(step - 2, 0)
-            if step == 1 + LAG:
-                for part in range(WE_PARTS):
-                    round_we(nc.vector.tensor_copy if part < 0 else nc.scalar.copy, 1, part)
-                for part in range(WE_PARTS):
-                    quantise_we(1, part)
-            if 0 <= step - 2 - LAG:
-                evaluate(step - 2 - LAG, 1)
-            if 0 <= step - 1 < UNITS:
-                combine(step - 1)
+        def prepare_we(g):
+            for part in range(2):
+                round_we(nc.vector.tensor_copy if (g, part) in WE_VECTOR else nc.scalar.copy, g, part)
+            for part in range(2):
+                quantise_we(g, part)
 
-        blocks = [(q, g) for q in range(PIECES) for g in range(GROUPS)]
-        for step in range(len(blocks) + 1):
-            if step < len(blocks):
-                round_y(*blocks[step])
-            if step > 0:
-                quantise_y(*blocks[step - 1])
+        multiply(0,512)
+        prepare_we(0)
+        round_h(0)
+        round_h(1)
+        quantise_h(0)
+        quantise_h(1)
+        prepare_we(1)
+        multiply(512,512)
+        evaluate(0,0,512)
+        evaluate(1,0,512)
+        round_h(2)
+        round_h(3)
+        quantise_h(2)
+        quantise_h(3)
+        evaluate(0,512,512)
+        evaluate(1,512,512)
+        round_y(0,0)
+        round_y(1,0)
+        quantise_y(0,0)
+        quantise_y(1,0)
+        store_codes(0,0,2)
+        round_y(0,1)
+        round_y(1,1)
+        quantise_y(0,1)
+        quantise_y(1,1)
+        store_codes(1,0,2)
+        round_y(2,0)
+        round_y(3,0)
+        quantise_y(2,0)
+        quantise_y(3,0)
+        store_codes(0,2,4)
+        round_y(2,1)
+        round_y(3,1)
+        quantise_y(2,1)
+        quantise_y(3,1)
+        store_codes(1,2,4)
+        store_scales()

from contextlib import ExitStack

import concourse.mybir as mybir
from concourse.masks import make_identity

K, T, S, H, N = 1024, 2048, 1024, 512, 1024
FLOPS = 2 * (2 * K * H * S + H * N * S)

F32 = mybir.dt.float32
BF16 = mybir.dt.bfloat16
I32 = mybir.dt.int32
U32 = mybir.dt.uint32
U16 = mybir.dt.uint16
U8 = mybir.dt.uint8
FP8X4 = mybir.dt.float8_e4m3fn_x4
FP4X4 = mybir.dt.float4_e2m1fn_x4
ALU = mybir.AluOpType
RELU = mybir.ActivationFunctionType.Relu

P = 128
PACK = 4
K_PASS = P * PACK
PASSES = K // K_PASS
GROUPS = N // K_PASS
HALF = S // 2
BANK = 512
ROW0 = 96
WIDTHS = (512, 512)
STARTS = [sum(WIDTHS[:q]) for q in range(len(WIDTHS))]
PIECES = len(WIDTHS)
BLOCK = 256
STORE_SLOTS = 1
CODE_STORES = {1: 0, 3: 2}
SCALE_STORES = {3: 0}
SCALAR_ROUNDS = ((2, 1),)
WP_VECTOR = (4, 4)
WE_VECTOR = ()
OWN_VECTOR = ()


def tile_list_clamped_pair_eval_kernel(
    tc, tab_words, tab_scales, tab2_words, tab2_scales, offs, offs2, wo_words, wo_scales, wp, cap, we, out_0, out_1, out_2
):
    nc = tc.nc
    with ExitStack() as ctx:
        lists = ctx.enter_context(tc.tile_pool(name="lists", bufs=1))
        keep = ctx.enter_context(tc.tile_pool(name="keep", bufs=1))
        psum = ctx.enter_context(tc.psum_pool(name="psum", bufs=4))

        offsets = [lists.tile([P, S // 16], U16, name=f"offsets{s}") for s in range(2)]
        scale_window = [keep.tile([P, T], U8, name=f"scale_window{s}", align_bytes=64) for s in range(2)]
        scale_picked = [keep.tile([P, S], U8, name=f"scale_picked{s}", align_bytes=64) for s in range(2)]
        v_plane = keep.tile([P, PASSES * S], U8, name="v_plane", align_bytes=64)
        word_window = [[keep.tile([P, T], U32, name=f"word_window{s}{a}", align_bytes=64) for a in range(PASSES)] for s in range(2)]
        v_words = [[keep.tile([P, S], U32, name=f"v_words{s}{a}", align_bytes=64) for a in range(PASSES)] for s in range(2)]
        wo_raw = keep.tile([P, PASSES * 2 * H], U8, name="wo_raw", align_bytes=64)
        wo_scale_raw = keep.tile([P, PASSES * H], U8, name="wo_scale_raw", align_bytes=64)
        wo_codes = keep.tile([P, PASSES * 2 * H], U8, name="wo_codes", align_bytes=64)
        wo_plane = keep.tile([P, PASSES * H], U8, name="wo_plane", align_bytes=64)
        wp_raw = [keep.tile([P, PACK, H], F32, name=f"wp_raw{a}") for a in range(PASSES)]
        wp_round = [keep.tile([P, PACK * H], BF16, name=f"wp_round{a}", align_bytes=64) for a in range(PASSES)]
        wp_codes = [keep.tile([P, H], U32, name=f"wp_codes{a}", align_bytes=64) for a in range(PASSES)]
        wp_plane = [keep.tile([P, H], U8, name=f"wp_plane{a}", align_bytes=64) for a in range(PASSES)]
        we_raw = [keep.tile([P, PACK, K_PASS], F32, name=f"we_raw{g}") for g in range(GROUPS)]
        we_round = [[keep.tile([P, 2 * K_PASS], BF16, name=f"we_round{g}{part}", align_bytes=64) for part in range(2)] for g in range(GROUPS)]
        we_codes = [keep.tile([P, K_PASS], U32, name=f"we_codes{g}", align_bytes=64) for g in range(GROUPS)]
        we_plane = [keep.tile([P, K_PASS], U8, name=f"we_plane{g}", align_bytes=64) for g in range(GROUPS)]
        identity = keep.tile([P, P], F32, name="identity")
        cap_rows = keep.tile([P, P], F32, name="cap_rows")
        cap_col = keep.tile([P, PACK], F32, name="cap_col")
        own = [keep.tile([P, PACK, HALF], F32, name=f"own{hf}") for hf in range(2)]
        product = [keep.tile([P, PACK, HALF], F32, name=f"product{hf}", tag="product") for hf in range(2)]
        h_round = [keep.tile([P, PACK * BLOCK], BF16, name=f"h_round{b}", align_bytes=64) for b in range(S // BLOCK)]
        h_codes = keep.tile([P, S], U32, name="h_codes", align_bytes=64)
        h_plane = keep.tile([P, S], U8, name="h_plane", align_bytes=64)
        y_full = [[keep.tile([P, PACK, HALF], F32, name=f"y_full{hf}{g}") for g in range(GROUPS)] for hf in range(2)]
        y_round = [[keep.tile([P, PACK * BLOCK], BF16, name=f"y_round{b}{g}", align_bytes=64) for g in range(GROUPS)] for b in range(S // BLOCK)]
        y_codes = [keep.tile([P, S], U32, name=f"y_codes{g}", align_bytes=64) for g in range(GROUPS)]
        y_plane = keep.tile([P, GROUPS * S], U8, name="y_plane", align_bytes=64)

        words_in = (tab_words, tab2_words)

        def load_words(s, a):
            nc.sync.dma_start(word_window[s][a][:].bitcast(I32), words_in[s][a].rearrange("p t i -> p (t i)").bitcast(I32))

        def load_wp(a):
            nc.sync.dma_start(wp_raw[a][:], wp[a * K_PASS : (a + 1) * K_PASS, :].rearrange("(p j) c -> p j c", j=PACK))

        def load_we(g):
            rows = we.rearrange("(q j i) n -> j q i n", j=PACK, i=8)
            for j in range(PACK):
                nc.sync.dma_start(we_raw[g][:, j, :], rows[j][:, :, g * K_PASS : (g + 1) * K_PASS])

        def gather_scales(s):
            nc.vector.tensor_copy(scale_picked[s][:], scale_window[s][:].indirect(offsets[s][:]))

        def gather_words(s, a):
            for hf in range(2):
                cols = slice(hf * HALF // 16, (hf + 1) * HALF // 16)
                nc.vector.tensor_copy(v_words[s][a][:, hf * HALF : (hf + 1) * HALF], word_window[s][a][:].indirect(offsets[s][:, cols]))

        def round_wp(copy, a, t):
            copy(
                wp_round[a][:].rearrange("p (t q h i j) -> p t q h j i", t=PACK, h=2, i=4, j=PACK)[:, t],
                wp_raw[a][:].rearrange("p j (q t h i) -> p t q h j i", t=PACK, h=2, i=4)[:, t],
            )

        def round_we(copy, g, part):
            ts = slice(2 * part, 2 * part + 2)
            copy(
                we_round[g][part][:].rearrange("p (t m j) -> p m j t", t=2, j=PACK),
                we_raw[g][:].rearrange("p j (m t) -> p m j t", t=PACK)[:, :, :, ts],
            )

        def quantise_we(g, part):
            cols = slice(2 * part * P, (2 * part + 2) * P)
            quantise(we_codes[g][:, cols], we_plane[g][:, cols], we_round[g][part][:])

        def quantise(codes, plane, values):
            nc.vector.quantize_mx(out=codes.bitcast(FP8X4), scales=plane, in_=values)

        def own_side(hf):
            cols = slice(hf * HALF, (hf + 1) * HALF)
            for t in range(PACK):
                bank = psum.tile([P, BANK], F32, name="project_bank")
                for a in range(PASSES):
                    lo = a * H + t * P
                    nc.tensor.matmul_mx(
                        out=bank[:],
                        lhsT=wo_codes[:, 2 * lo : 2 * (lo + P)].bitcast(FP4X4),
                        lhsT_scale=wo_plane[:, lo : lo + P],
                        rhs=v_words[0][a][:, cols].bitcast(FP8X4),
                        rhs_scale=v_plane[:, a * S + cols.start : a * S + cols.stop],
                        start=(a == 0),
                        stop=(a == PASSES - 1),
                    )
                if (hf, t) in OWN_VECTOR:
                    nc.vector.tensor_scalar(out=own[hf][:, t, :], in0=bank[:], scalar1=0.0, scalar2=1.0, op0=ALU.max, op1=ALU.min)
                else:
                    nc.scalar.activation(own[hf][:, t, :], bank[:], RELU, bias=1.0, scale=-1.0)
            first = len([t for t in range(PACK) if (hf, t) in OWN_VECTOR])
            if first < PACK:
                nc.scalar.activation(own[hf][:, first:PACK, :], own[hf][:, first:PACK, :], RELU, bias=1.0, scale=-1.0)

        def multiply(start, width):
            cols = slice(start, start + width)
            hf, c0 = divmod(start, HALF)
            slots = BANK // width
            for t0 in range(0, PACK, slots):
                bank = psum.tile([P, slots, width], F32, name="project_bank")
                for e in range(slots):
                    t = t0 + e
                    for a in range(PASSES):
                        nc.tensor.matmul_mx(
                            out=bank[:, e, :],
                            lhsT=wp_codes[a][:, t * P : (t + 1) * P].bitcast(FP8X4),
                            lhsT_scale=wp_plane[a][:, t * P : (t + 1) * P],
                            rhs=v_words[1][a][:, cols].bitcast(FP8X4),
                            rhs_scale=scale_picked[1][4 * a : P, cols],
                            start=(a == 0),
                            stop=(a == PASSES - 1),
                        )
                for e in range(slots):
                    t = t0 + e
                    nc.vector.scalar_tensor_tensor(
                        out=product[hf][:, t, c0 : c0 + width],
                        in0=bank[:, e, :],
                        scalar=cap_col[:, t : t + 1],
                        in1=own[hf][:, t, c0 : c0 + width],
                        op0=ALU.min,
                        op1=ALU.mult,
                    )

        def round_h(b):
            hf, c0 = divmod(b * BLOCK, HALF)
            nc.vector.tensor_scalar(
                out=h_round[b][:].rearrange("p (c i t) -> p c t i", t=PACK, i=4),
                in0=product[hf][:, :, c0 : c0 + BLOCK].rearrange("p t (c i) -> p c t i", i=4),
                scalar1=0.0,
                scalar2=None,
                op0=ALU.max,
            )

        def quantise_h(b):
            cols = slice(b * BLOCK, (b + 1) * BLOCK)
            quantise(h_codes[:, cols], h_plane[:, cols], h_round[b][:])

        def evaluate(g, start, width):
            cols = slice(start, start + width)
            hf, c0 = divmod(start, HALF)
            slots = BANK // width
            rows = out_0[g * K_PASS : (g + 1) * K_PASS, cols].rearrange("(p t) c -> p t c", t=PACK)
            for t0 in range(0, PACK, slots):
                bank = psum.tile([P, slots, width], F32, name="evaluate_bank")
                for e in range(slots):
                    t = t0 + e
                    nc.tensor.matmul_mx(
                        out=bank[:, e, :],
                        lhsT=we_codes[g][:, t * P : (t + 1) * P].bitcast(FP8X4),
                        lhsT_scale=we_plane[g][:, t * P : (t + 1) * P],
                        rhs=h_codes[:, cols].bitcast(FP8X4),
                        rhs_scale=h_plane[:, cols],
                        start=True,
                        stop=True,
                    )
                result = y_full[hf][g][:, t0 : t0 + slots, c0 : c0 + width]
                nc.scalar.copy(result, bank[:])
                nc.sync.dma_start(rows[:, t0 : t0 + slots, :], result)

        def round_y(b, g):
            hf, c0 = divmod(b * BLOCK, HALF)
            copy = nc.scalar.copy if (b, g) in SCALAR_ROUNDS else nc.vector.tensor_copy
            copy(
                y_round[b][g][:].rearrange("p (c i t) -> p c t i", t=PACK, i=4),
                y_full[hf][g][:, :, c0 : c0 + BLOCK].rearrange("p t (c i) -> p c t i", i=4),
            )

        def quantise_y(b, g):
            cols = slice(b * BLOCK, (b + 1) * BLOCK)
            quantise(y_codes[g][:, cols], y_plane[:, g * S + cols.start : g * S + cols.stop], y_round[b][g][:])

        def store_codes(g, first, last):
            done = slice(first * BLOCK, last * BLOCK)
            nc.sync.dma_start(out_1[g].rearrange("p m t -> p (m t)").bitcast(I32)[:, done], y_codes[g][:, done].bitcast(I32))

        def store_scales():
            rows = out_2.bitcast(I32).rearrange("g (quad r) w -> r quad g w", r=4)
            for r in range(4):
                queue = nc.scalar if r % 2 == 1 else nc.sync
                queue.dma_start(rows[r], y_plane[r:P:32, :].bitcast(I32).rearrange("p (g w) -> p g w", g=GROUPS))

        def load_tab2_scales():
            for quad in range(4):
                nc.sync.dma_start(
                    scale_window[1][32 * quad : 32 * quad + 8, :].bitcast(I32), tab2_scales.bitcast(I32)[:, 4 * quad : 4 * quad + 4, :]
                )

        def load_wo_scales():
            rows = wo_scales.bitcast(I32).rearrange("a (quad r) w -> r quad a w", r=4)
            for r in range(4):
                nc.sync.dma_start(wo_scale_raw[r:P:32, :].bitcast(I32).rearrange("p (a w) -> p a w", a=PASSES), rows[r])

        def load_cap():
            nc.sync.dma_start(cap_rows[0:PACK, :].rearrange("t (q i) -> t q i", i=8), cap.rearrange("(q t i) -> t q i", t=PACK, i=8))

        def load_wo():
            nc.sync.dma_start(
                wo_raw[:].bitcast(I32).rearrange("p (a w) -> p a w", a=PASSES), wo_words.bitcast(I32).rearrange("a p w -> p a w")
            )

        def place_scales():
            for r in range(4):
                nc.sync.dma_start(
                    v_plane[r:P:32, :].bitcast(I32).rearrange("p (a w) -> p a w", a=PASSES),
                    scale_picked[0][ROW0 + 8 * r : ROW0 + 8 * r + 8, :].bitcast(I32),
                )

        def deal_wo():
            for dealt, raw, run in ((wo_plane, wo_scale_raw, 2), (wo_codes, wo_raw, 4)):
                nc.vector.tensor_copy(
                    dealt[:].bitcast(I32).rearrange("p (a t q w) -> p a t q w", a=PASSES, t=PACK, w=run),
                    raw[:].bitcast(I32).rearrange("p (a q t w) -> p a t q w", a=PASSES, t=PACK, w=run),
                )

        nc.vector.memset(scale_window[1][:].bitcast(I32), 0)
        nc.vector.memset(wo_scale_raw[:].bitcast(I32), 0)
        nc.vector.memset(scale_window[0][0:ROW0, :].bitcast(I32), 0)
        nc.vector.memset(v_plane[:].bitcast(I32), 0)
        nc.vector.memset(cap_rows[:], 0.0)
        make_identity(nc, identity[:])

        nc.sync.dma_start(offsets[0][:], offs)
        for a in range(PASSES):
            nc.sync.dma_start(
                scale_window[0][ROW0 + a : P : 2, :].bitcast(I32), tab_scales[a].bitcast(I32).rearrange("(quad r) w -> r quad w", r=4)
            )
        nc.sync.dma_start(offsets[1][:], offs2)
        load_tab2_scales()
        load_words(0, 0)
        load_wo_scales()
        load_cap()
        load_wo()
        load_words(0, 1)
        gather_scales(0)
        place_scales()
        load_wp(0)
        load_words(1, 0)
        load_wp(1)
        load_words(1, 1)
        load_we(0)
        load_we(1)

        gather_scales(1)
        cap_bank = psum.tile([P, P], F32, name="project_bank")
        nc.tensor.transpose(cap_bank[:], cap_rows[:], identity[:])
        nc.scalar.copy(cap_col[:], cap_bank[:, 0:PACK])
        gather_words(0, 0)
        deal_wo()
        gather_words(0, 1)
        for hf in range(2):
            own_side(hf)
        for a in range(PASSES):
            for t in range(PACK):
                round_wp(nc.vector.tensor_copy if t < WP_VECTOR[a] else nc.scalar.copy, a, t)
            for t in (0, 2):
                quantise(wp_codes[a][:, t * P : (t + 2) * P], wp_plane[a][:, t * P : (t + 2) * P], wp_round[a][:, t * K_PASS : (t + 2) * K_PASS])
            gather_words(1, a)

        def prepare_we(g):
            for part in range(2):
                round_we(nc.vector.tensor_copy if (g, part) in WE_VECTOR else nc.scalar.copy, g, part)
            for part in range(2):
                quantise_we(g, part)

        multiply(0,512)
        prepare_we(0)
        round_h(0)
        round_h(1)
        quantise_h(0)
        quantise_h(1)
        prepare_we(1)
        multiply(512,512)
        evaluate(0,0,512)
        evaluate(1,0,512)
        round_h(2)
        round_h(3)
        quantise_h(2)
        quantise_h(3)
        evaluate(0,512,512)
        evaluate(1,512,512)
        round_y(0,0)
        round_y(1,0)
        quantise_y(0,0)
        quantise_y(1,0)
        store_codes(0,0,2)
        round_y(0,1)
        round_y(1,1)
        quantise_y(0,1)
        quantise_y(1,1)
        store_codes(1,0,2)
        round_y(2,0)
        round_y(3,0)
        quantise_y(2,0)
        quantise_y(3,0)
        store_codes(0,2,4)
        round_y(2,1)
        round_y(3,1)
        quantise_y(2,1)
        quantise_y(3,1)
        store_codes(1,2,4)
        store_scales()
